import numpy as np, ml_dtypes
CORES = [25,29,65,69,153,157,193,197]
N = 8
import mx_ref
BF = ml_dtypes.bfloat16
def gentries(a):
    return np.ascontiguousarray(a.reshape(8, 16, -1).transpose(0, 2, 1)).reshape(8, -1)
def gtable(e):
    e = np.asarray(e); return np.ascontiguousarray(e.reshape(8, -1, 16).transpose(0, 2, 1)).reshape(128, -1).astype(np.int32)
def gcols(t, e):
    v = np.concatenate([t.reshape(8, 16, -1, 4), np.zeros((8, 16, 1, 4), BF)], axis=2)
    return np.ascontiguousarray(np.stack([v[g][:, e[g]] for g in range(8)])).reshape(128, -1)
def tile(rs):
    return np.stack(rs, axis=2).reshape(128, -1).astype(BF)
def pick(q, e):
    c = np.concatenate([q[0].reshape(128, -1, 4), np.zeros((128, 1, 4), np.uint8)], axis=1); s = np.concatenate([q[1], np.ones((16, 1), np.uint8)], axis=1)
    return (np.ascontiguousarray(c[:, e].reshape(128, -1)), np.ascontiguousarray(s[:, e]))
def join(*qs):
    return (np.concatenate([q[0] for q in qs], axis=1), np.concatenate([q[1] for q in qs], axis=1))
def put(q, e, v):
    c, s = q[0].reshape(128, -1, 4).copy(), q[1].copy(); c[:, e] = v[0].reshape(128, -1, 4); s[:, e] = v[1]
    return (c.reshape(128, -1), s)
def pk(c, s):
    return (np.ascontiguousarray(c), mx_ref.live(s))
def emit(q):
    return q[0], q[1]
def packed(v, rng):
    q = [mx_ref.quantize(np.ascontiguousarray(v[r])) for r in range(N)]
    return np.stack([a for a, b in q]), np.stack([mx_ref.plane(b, rng) for a, b in q])
def values_of_codes():
    e, c = np.zeros((128, 128, 4), np.float32), np.zeros((128, 2, 4), np.uint8)
    e[np.arange(128), np.arange(128), 0] = 1
    c[:127, :, 0] = np.arange(256).reshape(2, 128).T[:127]
    return mx_ref.matmul(mx_ref.quantize(e.reshape(128, 512).astype(BF)), (c.reshape(128, 8), np.full((16, 2), 127, np.uint8))).T.reshape(-1).astype(np.float64)
CODE_VALUE, SCALE_VALUE = values_of_codes(), 2.0 ** (np.arange(256) - 127.0)
def decode(q):
    return (CODE_VALUE[q[0]].reshape(16, 8, -1, 4) * SCALE_VALUE[q[1]][:, None, :, None] + 0.0).reshape(128, -1).astype(np.float32)
def f(rng, *shape):
    return mx_ref.flush((rng.standard_normal(shape, dtype=np.float32) * np.exp2(rng.integers(-2, 3, shape[:-1] + (1,)))).astype(BF))
def wide(rng, *shape, cols=0):
    v = rng.standard_normal(shape, dtype=np.float32) * np.exp2(rng.integers(-12, 13, shape)).astype(np.float32)
    if cols: v *= np.repeat(np.exp2(rng.integers(-cols, cols + 1, shape[:-2] + (1, shape[-1] // 4))) * (rng.random(shape[:-2] + (1, shape[-1] // 4)) > 0.0625), 4, axis=-1).astype(np.float32)
    return mx_ref.flush(v.astype(BF))
C = 288
STEP = [4, 1, 2]
def take(a, e):
    return np.take_along_axis(a, e, axis=-1)
def effective(back):
    e = np.ones(back.shape, bool)
    for j in range(C - 1, -1, -1):
        up = back[..., j]
        e[..., j] = (up <= j) | ~take(e, up[..., None])[..., 0]
    return e
def numbers_of(rng):
    return {"x": np.array(f(rng, N, 128, 4 * C)), "u": np.array(f(rng, N, 128, 512)), "v": np.array(f(rng, N, 128, 512))}
def stored(back, ring, mate):
    return {k: np.stack([gtable(e[r]) for r in range(N)]) for k, e in (("ud", np.argsort(back, axis=-1)), ("iv", back), ("hp", ring), ("mt", mate))}
def shuffled(rng):
    return rng.permuted(np.tile(np.arange(C), (N, 8, 1)), axis=2)
def linked(order):
    e = np.zeros_like(order)
    np.put_along_axis(e, order, np.roll(order, -1, axis=-1), axis=-1)
    return e
def mates(rng):
    a = shuffled(rng)
    e = np.zeros_like(a)
    np.put_along_axis(e, a[..., ::2], a[..., 1::2], axis=-1)
    np.put_along_axis(e, a[..., 1::2], a[..., ::2], axis=-1)
    return e
def runs(rng, back):
    return linked(np.argsort(effective(back) + rng.random(back.shape), axis=-1))
def lists(rng):
    return stored(shuffled(rng), linked(shuffled(rng)), mates(rng))
def layers(rng, still=()):
    w = np.array(f(rng, N, 128, 2048)).reshape(N, 8, 16, 4, 8, 16, 4)
    for i in still:
        w[:, :, i] = 0
        w[:, :, :, :, :, i] = 0
    return w
def weights(rng, w):
    c, s = packed(np.ascontiguousarray(w).reshape(N, 128, 2048), rng)
    return {"wc": c, "ws": s}
def setup_inputs(rng):
    return {**numbers_of(rng), **lists(rng), **weights(rng, layers(rng))}
def setup_inputs_ties(rng):
    d = numbers_of(rng)
    o = rng.permutation(N)
    k = rng.choice([-1.0, 0.0, 1.0, 1.0], (N, 8, C))
    k[o[0]] = 0
    k[o[1]] = 1
    k[o[2]] = (rng.permutation(8) % 2 * 2.0 - 1.0)[:, None]
    x = d["x"].reshape(N, 8, 16, C, 4)
    x[:, :, 0] = 0
    x[:, :, 0, :, 0] = k.astype(np.float32).astype(BF)
    u = d["u"].reshape(N, 128, 128, 4)
    u[:, :, ::16] = 0
    for h in range(0, 128, 16): u[:, h, h, 0] = 1
    back = np.zeros((N, 8, C), np.int64)
    for r in range(N):
        for g, m in enumerate(rng.permutation([1, 1, 1, 2, 2, 3, C // 8, 0])):
            a = rng.integers(0, m, C) if m else np.arange(C)
            for i in np.unique(a):
                e = np.flatnonzero(a == i)
                back[r, g, e] = np.roll(e, -1)
    mate = mates(rng)
    tau = np.where((k > 0) & (take(k, mate) > 0), mate, np.arange(C))
    return {"x": x.reshape(N, 128, 4 * C), "u": u.reshape(N, 128, 512), "v": d["v"], **stored(take(tau, back), runs(rng, back), mate), **weights(rng, layers(rng, [0]))}
def setup_inputs_near(rng):
    d = numbers_of(rng)
    i = np.arange(N)
    first = np.minimum(i, i ^ STEP[0])
    small = np.isin(first, rng.permutation(np.unique(first))[:N // 4])
    k = np.where(small, 2.0 ** -30, 1.0)
    x = d["x"].astype(np.float32).reshape(N, 8, 16, C, 4)
    x[:, :, :8] = 0
    s = rng.choice([-1.0, 0.0, 1.0, 1.0], (N, 8, C)) * k[:, None, None]
    x[:, :, 0, :, 0] = 1.125 * s
    x[:, :, 1, :, 0] = -1.25 * s
    x[:, :, 3, :, 0] = np.where(small[:, None, None], rng.choice([-1.0, 1.0], (N, 8, C)) * 2.0 ** -30, 0.0)
    x[:, :, 4, :, 0] = np.where(small, 2.0 ** -27, 0.0)[:, None, None]
    u = d["u"].reshape(N, 128, 128, 4)
    u[:, :, ::16] = 0
    w = layers(rng, range(8))
    for r in range(N):
        at = [0, C - 1, int(rng.integers(C)), int(rng.integers(C))]
        for g, j in zip(rng.permutation(8)[:4], at): x[r, g, 0, j, 0] = 2.0 ** 30 * rng.choice([-1.0, 1.0])
        for g in range(8):
            h = 16 * g
            u[r, h, h, 0] = 1.125 * k[r]
            u[r, h + 1, h, 0] = k[r]
            u[r, h + 2, h, 0] = 1.125 * k[r]
            u[r, h + 5, h, 0] = k[r]
            if small[r]:
                w[r, g, 3, 0, g, 2, 0] = 2.0 ** -7
                w[r, g, 3, 0, g, 5, 0] = -2.0 ** -7
    return {"x": x.reshape(N, 128, 4 * C).astype(BF), "u": u.reshape(N, 128, 512), "v": d["v"], **lists(rng), **weights(rng, w)}
def setup_inputs_odd(rng):
    d = numbers_of(rng)
    x = (1.0 + (2 * rng.integers(0, 64, (N, 16, 8, C, 4)) + 1) * 2.0 ** -7) * np.exp2(-rng.integers(0, 7, (N, 16, 8, C, 4)).astype(np.float64)) * rng.choice([-1.0, 1.0], (N, 16, 8, C, 4))
    x[:, ::2] = 0
    x[:, :, 0, :, 0] = 1.96875 * 2.0 ** 8 * rng.choice([-1.0, 1.0], (N, 16, C))
    x[:, ::2, 1, :, 0] = (1.0 + 0.125 * (rng.random((N, 8, C)) < 0.75)) * 2.0 ** -5
    x[:, ::2, 2, :, 0] = (1.0 + 0.125 * (rng.random((N, 8, C)) < 0.25)) * 2.0 ** -5
    x[:, 14, 0, :, 1] = 16.0
    u = d["u"].reshape(N, 128, 128, 4)
    u[:, :, ::16] = 0
    for h in range(0, 128, 16):
        u[:, h + 1, h, 0] = 1
        u[:, h + 2, h, 0] = -1
        u[:, h + 3, h, 0] = 1
    w = layers(rng, [0, 1, 2, 8])
    w[:, 7, 0, 0, :, 0, 1] = -16.0
    return {"x": x.astype(np.float32).reshape(N, 128, 4 * C).astype(BF), "u": u.reshape(N, 128, 512), "v": d["v"], **lists(rng), **weights(rng, w)}
def setup_inputs_ends(rng):
    d = numbers_of(rng)
    x = np.zeros((N, 8, 16, C, 4))
    u = d["u"].astype(np.float32).reshape(N, 128, 128, 4)
    v = d["v"].astype(np.float32)
    w = np.zeros((N, 128, 4, 128, 4), np.float32)
    o, kinds = np.zeros(N, np.int64), rng.permutation(4)
    left = rng.permutation(np.unique(np.minimum(np.arange(N), np.arange(N) ^ STEP[0])))
    o[left] = kinds[:N // 2]
    o[left ^ STEP[0]] = kinds[(np.arange(N // 2) + 2) % 4]
    i, j = np.arange(128), np.arange(C)
    turns = np.stack([j ^ 1, C - 1 - j, (j + C // 2) % C])
    ways = np.stack([np.roll(j, -1), j, C - 1 - j, np.roll(j, 1)])
    mate = np.stack([turns[rng.permutation(8) % 3] for r in range(N)])
    plan = np.stack([ways[rng.permutation(8) % 4] for r in range(N)])
    ring, back = runs(rng, plan), plan.copy()
    for r in range(N):
        h = rng.permutation(8)
        sign = np.where(h < 2, 0.0, h % 2 * 2.0 - 1.0)
        c = sign[None, :, None]
        e = rng.permutation(8)
        ring[r, e[:2]] = np.roll(j, -1)
        ring[r, e[2:4]] = np.roll(j, 1)
        if o[r] in (0, 2): back[r, sign < 0] = take(mate[r], plan[r])[sign < 0]
        low = -(0.9 + 0.1 * rng.random((8, 16, C, 4))) * 2.0 ** 30
        if o[r] == 0: x[r] = low
        if o[r] == 1: x[r] = np.where((rng.random(C) < 0.5)[:, None], (1.0 + 0.4 * rng.random((8, 16, C, 4))) * 2.0 ** 27, low)
        if o[r] == 2: x[r] = -(1.0 + 0.125 * rng.integers(0, 8, (8, 16, C, 4))) * 2.0 ** -30
        if o[r] == 3: x[r] = d["x"][r].astype(np.float32).reshape(8, 16, C, 4)[:, :, :1]
        if o[r] < 2:
            x[r, 7, 15, :, 3] *= 2.0 ** -6
            u[r, :, ::16] = c * (0.9 + 0.1 * rng.random((128, 8, 4))) * 2.0 ** 30
            v[r] = rng.choice([-1.0, 1.0], (128, 512)) * (0.9 + 0.1 * rng.random((128, 512))) * 2.0 ** 30
        if o[r] == 2:
            u[r, :, ::16] = c * (1.0 + 0.125 * rng.integers(0, 8, (128, 8, 4))) * 2.0 ** -30
            v[r] = rng.choice([-1.0, 1.0], (128, 512)) * (1.0 + 0.125 * rng.integers(0, 8, (128, 512))) * 2.0 ** -30
        if o[r] == 3: u[r, :, ::16] *= np.abs(c).astype(np.float32)
        k = np.array([8.0, 16.0, 32.0])[rng.permutation(8) % 3]
        for b in range(4): w[r, i, b, i, b] = k[i // 16]
        if o[r] == 2:
            w[r, 127, 3, 127, 3] = 256.0
            w[r, 126, 3, 126, 3] = 2.0 ** -8
    return {"x": x.astype(np.float32).reshape(N, 128, 4 * C).astype(BF), "u": u.reshape(N, 128, 512).astype(BF), "v": v.astype(BF), **stored(back, ring, mate), **weights(rng, w.astype(BF))}
def setup_inputs_spread(rng):
    d = setup_inputs(rng)
    d["x"] = wide(rng, N, 128, 4 * C, cols=6)
    return d
def check_inputs(d):
    b = []
    for k in ("x", "u", "v"):
        a = np.abs(d[k].astype(np.float32))
        if not (np.isfinite(a).all() and ((a == 0) | (a >= 2.0 ** -30) & (a <= 2.0 ** 30)).all()): b.append("a value of " + k)
    none, least, most = [emit(mx_ref.quantize(np.full((128, 16), k, np.float32).astype(BF)))[1][0, 0] for k in (0.0, 2.0 ** -8, 2.0 ** 8)]
    own = np.arange(C)
    for r in range(N):
        ud, iv, hp, mt = [gentries(d[k][r]) for k in ("ud", "iv", "hp", "mt")]
        if any(((a < 0) | (a >= C)).any() for a in (ud, iv, hp, mt)): b.append("an entry of a list")
        else:
            if (np.sort(ud, axis=1) != own).any(): b.append("ud: a permutation")
            if (take(ud, iv) != own).any(): b.append("iv: the inverse of ud")
            if (take(mt, mt) != own).any() or (mt == own).any(): b.append("mt: pairs of columns")
            at, seen = np.zeros((8, 1), np.int64), np.zeros((8, C), bool)
            for j in range(C):
                at = take(hp, at)
                np.put_along_axis(seen, at, True, axis=1)
            if not seen.all(): b.append("hp: a ring")
        if ((d["wc"][r] == 0x7F) | (d["wc"][r] == 0xFF)).any(): b.append("wc: a code that is no number")
        s = mx_ref.live(d["ws"][r])
        if ((s != none) & ((s < least) | (s > most))).any(): b.append("ws: a scale out of range")
    return b
def halfsum(s, t):
    return ((s.astype(np.float32) + t.astype(np.float32)) * np.float32(0.5)).astype(BF)
def reference(x, u, v, ud, iv, hp, mt, wc, ws):
    qu = [mx_ref.quantize(u[r]) for r in range(N)]
    lay = [pk(wc[r], ws[r]) for r in range(N)]
    to, back, ring, mate = [[gentries(a[r]) for r in range(N)] for a in (ud, iv, hp, mt)]
    now = [x[r] for r in range(N)]
    for step in STEP:
        t, past, sent = [], [], []
        for r in range(N):
            q = mx_ref.quantize(now[r])
            s = mx_ref.matmul(qu[r], q)[::16] > 0
            t.append(decode(q).astype(BF))
            tau = np.where(s & take(s, mate[r]), mate[r], np.arange(C))
            to[r], back[r] = take(to[r], tau), take(tau, back[r])
            e, b = effective(back[r]), ring[r]
            while not take(e, b).all(): b = np.where(take(e, b), b, take(ring[r], b))
            past.append(b)
            sent.append(mx_ref.quantize(halfsum(gcols(t[r], b), gcols(t[r], back[r]))))
        for r in range(N):
            p = r ^ step
            h = tile([mx_ref.matmul(pick(lay[r], np.arange(128 * b, 128 * b + 128)), sent[p]) * np.float32(0.03125) for b in range(4)])
            now[r] = halfsum(gcols(t[r], to[r]), gcols(h, take(past[p], back[r])))
    y, uo = np.zeros((N, 128, C), np.float32), np.zeros((N, 8, C), np.float32)
    oc, osc = np.zeros((N, 128, 4 * C), np.uint8), np.zeros((N, 16, C), np.uint8)
    for r in range(N):
        q = mx_ref.quantize(now[r])
        y[r] = mx_ref.matmul(mx_ref.quantize(v[r]), q)
        uo[r] = to[r]
        oc[r], osc[r] = emit(q)
    return {"y": y, "uo": uo, "oc": oc, "osc": osc}

@@ -1,0 +1,441 @@
+from concourse.mybir import dt, AluOpType, ActivationFunctionType
+
+C, KW = 288, 18
+STEP = (4, 1, 2)
+MID = 145
+BIG = 512.0
+SCAN = "float16"
+EARLY = (0, 1)
+
+SCRATCH = {}
+for _n in ("xin", "xt", "zt", "th", "tp", "tu", "gv", "hh"):
+    SCRATCH[_n] = ("sbuf", [128, 4 * C], "bfloat16")
+for _n in ("ut", "vt"):
+    SCRATCH[_n] = ("sbuf", [128, 512], "bfloat16")
+SCRATCH["et"] = ("sbuf", [128, 520], "bfloat16")
+for _n, _w in (("x0", C), ("x1", C), ("x2", C), ("x3", C), ("p0", C), ("p1", C), ("p2", C), ("z", C),
+               ("u", 128), ("ur", 128), ("v", 128), ("e", 512), ("w", 512)):
+    SCRATCH[_n + "q"] = ("sbuf", [128, _w], "float8_e4m3fn_x4")
+    SCRATCH[_n + "sc"] = ("sbuf", [128, _w], "uint8")
+for _n in ("iota", "win", "h1", "h2", "h4", "h8", "fl"):
+    SCRATCH[_n] = ("sbuf", [128, 304], "bfloat16")
+for _n in ("iom", "pat", "pp", "r1", "r2", "r3", "hx", "nf", "fo", "sa", "sb", "br", "uda", "udb", "mtr", "mr", "oo"):
+    SCRATCH[_n] = ("sbuf", [128, C], "bfloat16")
+SCRATCH["hpr"] = ("sbuf", [128, 9 * C], "bfloat16")
+for _n in ("c0", "c1", "c2", "c3"):
+    SCRATCH[_n] = ("sbuf", [128, C], SCAN)
+SCRATCH["pati"] = ("sbuf", [128, C], "int32")
+for _n in ("ivl", "mtl", "udl", "hpl"):
+    SCRATCH[_n] = ("sbuf", [128, KW], "int32")
+SCRATCH["qi"] = ("sbuf", [128, 8], "int32")
+for _n in ("corr", "thr", "qz"):
+    SCRATCH[_n] = ("sbuf", [128, 8], "float32")
+for _n in ("k16", "kb", "jw", "nbw", "mtw", "dtw", "t1", "bo", "td", "tw", "t3", "bj", "dj", "tf", "diw", "ndw", "ff", "di2"):
+    SCRATCH[_n] = ("sbuf", [128, KW], "float32")
+for _n in ("jw2", "im0", "im1", "ta", "tb", "nim"):
+    SCRATCH[_n] = ("sbuf", [128, 2 * KW], "float32")
+LOCAL = ("iv0", "mi", "mto", "udo", "wino", "off1", "poso", "tauo", "udi")
+SCRATCH["lloc"] = ("sbuf", [128, len(LOCAL) * KW], "uint16")
+for _n in ("iv1", "iv2", "iv3", "bo0", "bo1", "bo2", "eo0", "eo1", "eo2",
+           "ivp0", "ivp1", "ivp2", "bp0", "bp1", "bp2", "ep0", "ep1", "ep2", "hoff", "foff", "ordo"):
+    SCRATCH["l" + _n] = ("sbuf", [128, 4 * KW if _n == "hoff" else KW], "uint16")
+SCRATCH["lhp"] = ("sbuf", [128, 8 * KW], "uint16")
+SCRATCH["luo"] = ("sbuf", [128, 8], "uint16")
+SCRATCH["uoi"] = ("sbuf", [128, 8], "int32")
+SCRATCH["udf"] = ("sbuf", [128, C], "float32")
+SCRATCH["yf"] = ("sbuf", [128, C], "float32")
+SCRATCH["ps"] = ("psum", [128, 4096], "float32")
+
+SEMAPHORES = ["cv", "cs", "ct", "cg", "snt"] + ["d%d" % i for i in range(20)]
+SEMAPHORES += ["%s%d" % (a, i) for a in ("rx", "ri", "rb", "re") for i in range(3)]
+
+MUL, ADD, SUB, MAX, MIN = AluOpType.mult, AluOpType.add, AluOpType.subtract, AluOpType.max, AluOpType.min
+GT, GE, EQ = AluOpType.is_gt, AluOpType.is_ge, AluOpType.is_equal
+COPY, IDENT = ActivationFunctionType.Copy, ActivationFunctionType.Identity
+
+
+def relays(topo, src, dst):
+    if topo.may_write(src, dst):
+        return None
+    c = [a for a in topo.cores_of(src) if a != src and topo.may_write(a, dst)]
+    near = [a for a in c if topo.die(a) == topo.die(src)]
+    far = [a for a in c if topo.die(a) != topo.die(src)]
+    return (near + far)[:2]
+
+
+def rank_program(g, core, T, topo):
+    rank = T.rank_of(core)
+    sent = [0]
+
+    def put(dst, out, in_, sem):
+        e = topo.engines(core, dst)[:8]
+        rid, pid = topo.addr(dst, core)
+        m = 0
+        for a in e:
+            m |= 1 << a
+        g.remote_dma(out, in_, T.sem[sem], T.sem.snt, pid, rid, m)
+        sent[0] += len(e)
+        return len(e)
+
+    def width(a, b):
+        return len(topo.engines(a, b)[:8])
+
+    def u8(ap):
+        return ap.bitcast(dt.uint8)
+
+    HALF = C // 2
+    if rank is None:
+        for rd, step in enumerate(STEP):
+            for r, src in enumerate(T.cores):
+                dst = T.cores[r ^ step]
+                rel = relays(topo, src, dst)
+                if not rel or core not in rel:
+                    continue
+                n = width(src, core)
+                if core == rel[0]:
+                    g.wait_ge(T.sem["rx%d" % rd], 2 * n)
+                    put(dst, u8(T["p%dq" % rd][:, 0:HALF]), u8(T["p%dq" % rd][:, 0:HALF]), "rx%d" % rd)
+                    put(dst, T["p%dsc" % rd][:], T["p%dsc" % rd][:], "rx%d" % rd)
+                else:
+                    g.wait_ge(T.sem["rx%d" % rd], n)
+                    put(dst, u8(T["p%dq" % rd][:, HALF:C]), u8(T["p%dq" % rd][:, HALF:C]), "rx%d" % rd)
+                    for s, b in (("ri", "livp"), ("rb", "lbp"), ("re", "lep")):
+                        g.wait_ge(T.sem["%s%d" % (s, rd)], n)
+                        put(dst, T["%s%d" % (b, rd)][:], T["%s%d" % (b, rd)][:], "%s%d" % (s, rd))
+        if sent[0]:
+            g.wait_ge(T.sem.snt, sent[0])
+        return
+
+    Q = {"v": g.vector, "s": g.scalar, "t": g.tensor, "g": g, "y": g.sync}
+    SEM = {"v": "cv", "s": "cs", "t": "ct", "g": "cg"}
+    cnt = {"v": 0, "s": 0, "t": 0, "g": 0}
+    clock = {q: {} for q in Q}
+    wr, rdr = {}, {}
+    nd = [0]
+    dsems = []
+
+    def sync(q, reads, writes):
+        need = []
+        for k in reads:
+            if k in wr:
+                need.append(wr[k])
+        for k in writes:
+            if k in wr:
+                need.append(wr[k])
+            need += rdr.get(k, [])
+        need.sort(key=lambda t: -t[1])
+        for sem, val, clk in need:
+            if clock[q].get(sem, 0) < val:
+                Q[q].wait_ge(T.sem[sem], val)
+                for a, b in clk.items():
+                    if clock[q].get(a, 0) < b:
+                        clock[q][a] = b
+
+    def done(q, sem, val, reads, writes):
+        clk = dict(clock[q])
+        clk[sem] = val
+        tok = (sem, val, clk)
+        for k in reads:
+            rdr.setdefault(k, []).append(tok)
+        for k in writes:
+            wr[k] = tok
+            rdr[k] = []
+
+    def op(q, call, reads, writes):
+        sync(q, reads, writes)
+        i = call(Q[q])
+        cnt[q] += 1
+        i.then_inc(T.sem[SEM[q]], 1)
+        done(q, SEM[q], cnt[q], reads, writes)
+
+    def dma(q, out, in_, reads, writes):
+        sem = "d%d" % nd[0]
+        nd[0] += 1
+        sync(q, reads, writes)
+        Q[q].dma_start(out, in_).then_inc(T.sem[sem], 16)
+        dsems.append(sem)
+        done(q, sem, 16, reads, writes)
+
+    def tt(out, a, b, o, reads, writes):
+        op("v", lambda e: e.tensor_tensor(out, a, b, o), reads, writes)
+
+    def ts(out, a, s1, o1, reads, writes, s2=None, o2=None):
+        if o2 is None:
+            op("v", lambda e: e.tensor_scalar(out, a, s1, None, o1), reads, writes)
+        else:
+            op("v", lambda e: e.tensor_scalar(out, a, s1, s2, o1, o2), reads, writes)
+
+    def cp(out, in_, reads, writes, q="v"):
+        if q == "v":
+            op("v", lambda e: e.tensor_copy(out, in_), reads, writes)
+        else:
+            op("s", lambda e: e.activation(out, in_, COPY), reads, writes)
+
+    rot = [0]
+
+    def scan(row, n, key):
+        b = "c%d" % (rot[0] % 4)
+        rot[0] += 1
+        op("v", lambda e: e.tensor_tensor_scan(T[b][:, 0:n], row, T.pat[:, 0:n], -2 * BIG, MAX, ADD), [key, "pat"], [b])
+        return b, T[b][:, 15:n:16]
+
+    def wrap(row, n, key, off, okey):
+        b, e = scan(row, n, key)
+        ts(off, e, T.corr[:, 0:1], ADD, [b, "corr"], [okey])
+
+    def lst(name):
+        if name in LOCAL:
+            o = KW * LOCAL.index(name)
+            return T.lloc[:, o:o + KW]
+        return T["l" + name][:, 0:KW]
+
+    dma("s", T.hpl[:], T.hp[:], [], ["hpl"])
+    dma("y", T.xin[:], T.x[:], [], ["xin"])
+    dma("s", T.ivl[:], T.iv[:], [], ["ivl"])
+    dma("s", T.mtl[:], T.mt[:], [], ["mtl"])
+    dma("y", T.ut[:], T.u[:], [], ["ut"])
+    dma("s", T.udl[:], T.ud[:], [], ["udl"])
+    dma("y", u8(T.wq[:]), T.wc[:], [], ["wq"])
+    dma("y", T.wsc[:], T.ws[:], [], ["wsc"])
+    dma("y", T.vt[:], T.v[:], [], ["vt"])
+
+    op("v", lambda e: e.memset(T.lordo[:], 0), [], ["lordo"])
+    op("v", lambda e: e.memset(T.oo[:], float(-MID)), [], ["oo"])
+    op("g", lambda e: e.iota(T.qi[:], [[0, 8]], 0, 1), [], ["qi"])
+    op("g", lambda e: e.iota(T.pati[:], [[1, C]], 1024, -1), [], ["pati"])
+    op("g", lambda e: e.iota(T.iota[:], [[1, 304]], -MID, 0, allow_small_or_imprecise_dtypes=True), [], ["iota"])
+    op("v", lambda e: e.memset(T.et[:], 0.5), [], ["et"])
+    op("g", lambda e: e.iota(T.k16[:], [[16, KW]], 0, 0, allow_small_or_imprecise_dtypes=True), [], ["k16"])
+    op("g", lambda e: e.iota(T.kb[:], [[-32, KW // 2], [0, 2]], -32, 0, allow_small_or_imprecise_dtypes=True), [], ["kb"])
+    op("g", lambda e: e.iota(T.uoi[:], [[16, 8]], 0, 0), [], ["uoi"])
+    op("g", lambda e: e.iota(T.iom[:], [[1, C]], -1 - MID, 0, allow_small_or_imprecise_dtypes=True), [], ["iom"])
+    op("g", lambda e: e.affine_select(T.et[:], T.et[:], [[1, 520]], EQ, 0.0, -3, -4), ["et"], ["et"])
+    ts(T.qi[:], T.qi[:], 15, AluOpType.bitwise_and, ["qi"], ["qi"])
+    ts(T.qz[:], T.qi[:], 0.0, EQ, ["qi"], ["qz"])
+    ts(T.corr[:], T.qz[:], 2 * BIG, MUL, ["qz"], ["corr"], MID - BIG, ADD)
+    ts(T.pati[:], T.pati[:], 15, AluOpType.bitwise_and, ["pati"], ["pati"])
+    ts(T.pat[:], T.pati[:], 0.0, EQ, ["pati"], ["pat"], BIG, MUL)
+    ts(T.hx[:], T.pati[:], 15.0, EQ, ["pati"], ["hx"], -2 * BIG, MUL)
+    tt(T.pat[:], T.pat[:], T.hx[:], ADD, ["pat", "hx"], ["pat"])
+    cp(T.lhp[:, 0:KW], T.hpl[:], ["hpl"], ["lhp0"])
+    cp(T.hpr[:, 0:C], T.iota[:, 0:C].indirect(T.lhp[:, 0:KW]), ["iota", "lhp0"], ["hpr0"], "s")
+    cp(lst("iv0"), T.ivl[:], ["ivl"], ["liv0"])
+    cp(lst("mto"), T.mtl[:], ["mtl"], ["lmto"])
+    ts(T.thr[:], T.qz[:], -4 * BIG, MUL, ["qz"], ["thr"], 1.5 + 2 * BIG, ADD)
+    cp(T.jw[:, 0:1], T.qi[:, 0:1], ["qi"], ["jwq"])
+    ts(T.jw2[:, 0:KW], T.k16[:], T.jw[:, 0:1], ADD, ["k16", "jwq"], ["jwa"])
+    ts(T.jw2[:, KW:2 * KW], T.k16[:], T.jw[:, 0:1], ADD, ["k16", "jwq"], ["jwb"])
+    ts(T.nbw[:], T.kb[:], T.corr[:, 0:1], ADD, ["kb", "corr"], ["nbw"])
+    JW = T.jw2[:, 0:KW]
+    JK = ["jwa", "jwb"]
+
+    def ring(k):
+        a, b = (16, 18) if k < 6 or k == 8 else (14, 18) if k == 6 else (10, 18)
+        o = 0 if k == 8 else 16 * a - (1 << k)
+        cp(T.oo[:, o:o + 16 * (b - a)], T.hpr[:, k * C:(k + 1) * C].indirect(T.lordo[:, a:b]), ["hpr%d" % k, "lordo"], ["oo"], "s")
+        if k < 8:
+            cp(T.hpr[:, (k + 1) * C:(k + 2) * C], T.hpr[:, k * C:(k + 1) * C].indirect(T.lhp[:, k * KW:(k + 1) * KW]),
+               ["hpr%d" % k, "lhp%d" % k], ["hpr%d" % (k + 1)], "s")
+        s0, s1 = (256, 288) if k < 5 else (o, o + 16 * (b - a))
+        wrap(T.oo[:, s0:s1], s1 - s0, "oo", T.lordo[:, s0 // 16:s1 // 16], "lordo")
+        if k < 7:
+            wrap(T.hpr[:, (k + 1) * C:(k + 2) * C], C, "hpr%d" % (k + 1), T.lhp[:, (k + 1) * KW:(k + 2) * KW], "lhp%d" % (k + 1))
+
+    def ring_end():
+        cp(T.r1[:, 0:C].indirect(T.lordo[:, 0:KW]), T.iom[:], ["iom", "lordo"], ["r1"])
+        wrap(T.r1[:], C, "r1", lst("poso"), "lposo")
+
+    ring(0)
+    cp(T.mtr[:], T.iota[:, 0:C].indirect(lst("mto")), ["iota", "lmto"], ["mtr"], "s")
+    cp(T.mr[:], T.mtr[:].indirect(lst("iv0")), ["mtr", "liv0"], ["mr"], "s")
+    cp(T.im0[:, 0:KW], T.ivl[:], ["ivl"], ["im0"])
+    cp(T.mtw[:], T.mtl[:], ["mtl"], ["mtw"])
+    tt(T.dtw[:], T.mtw[:], JW, SUB, ["mtw"] + JK, ["dtw"])
+    cp(lst("udi"), T.udl[:], ["udl"], ["ludi"])
+
+    def prepare(rd):
+        im = "im%d" % (rd % 2)
+        b, e = scan(T.mr[:], C, "mr")
+        ts(T[im][:, KW:2 * KW], e, T.corr[:, 0:1], ADD, [b, "corr"], [im + "m"])
+        cp(lst("mi"), T[im][:, KW:2 * KW], [im + "m"], ["lmi"])
+        tt(T.ta[:], T[im][:], T.jw2[:], GT, [im, im + "m"] + JK, ["ta"])
+        ts(T.tb[:], T[im][:], float(C + 1), SUB, [im, im + "m"], ["tb"])
+        tt(T.diw[:], T[im][:, KW:2 * KW], T[im][:, 0:KW], SUB, [im, im + "m"], ["diw"])
+        tt(T.nim[:], T.ta[:], T.tb[:], MUL, ["ta", "tb"], ["nim"])
+        tt(T.ndw[:], T.nim[:, KW:2 * KW], T.nim[:, 0:KW], SUB, ["nim"], ["ndw"])
+        ts(T.nim[:], T.nim[:], float(C + 1), ADD, ["nim"], ["nim"])
+
+    for b in ("win", "h1", "h2", "h4", "h8"):
+        cp(T[b][:, C:C + 2], T.iota[:, C:C + 2], ["iota"], [b + "e"])
+    op("v", lambda e: e.memset(T.fl[:, C + 1:C + 2], 0.0), [], ["fle"])
+    op("v", lambda e: e.memset(T.fl[:, C:C + 1], 1.0), [], ["fl"])
+    op("v", lambda e: e.memset(T.iom[:, 0:1], float(C - 1 - MID)), ["iom"], ["iom"])
+    prepare(0)
+    op("v", lambda e: e.tensor_copy(T.luo[:], T.uoi[:]), ["uoi"], ["luo"])
+    op("v", lambda e: e.quantize_mx(T.x0q[:], T.x0sc[:], T.xin[:]), ["xin"], ["x0"])
+    ring(1)
+    op("v", lambda e: e.quantize_mx(T.uq[:], T.usc[:], T.ut[:]), ["ut"], ["u"])
+    op("v", lambda e: e.tensor_copy(T.urq[:, 0:128].bitcast(dt.uint32), T.uq[:, 0:128].bitcast(dt.uint32).indirect(T.luo[:, 0:8])),
+       ["u", "luo"], ["urq"])
+    op("s", lambda e: e.activation(T.ursc[:, 0:128], T.usc[:, 0:128].indirect(T.luo[:, 0:8]), COPY), ["u", "luo"], ["ursc"])
+
+    def mm(bank, l, ls, a, r, rs, reads):
+        op("t", lambda e: e.matmul_mx(T.ps[:, 512 * bank:512 * bank + C], T[l][:, a:a + 128], T[ls][:, a:a + 128], T[r][:, 0:C],
+                                      T[rs][:, 0:C], True, True), reads, ["b%d" % bank])
+
+    def bank(k):
+        return T.ps[:, 512 * k:512 * k + C]
+
+    def pl(name, b):
+        return T[name][:, b * C:(b + 1) * C]
+
+    ud = ["uda", "udb"]
+    for rd, step in enumerate(STEP):
+        xq, xs = "x%dq" % rd, "x%dsc" % rd
+        dst = T.cores[rank ^ step]
+        rel = relays(topo, core, dst)
+        backrel = relays(topo, dst, core)
+        RX, RI, RB, RE = ["%s%d" % (a, rd) for a in ("rx", "ri", "rb", "re")]
+        pq, pks = "p%dq" % rd, "p%dsc" % rd
+
+        def extra(k):
+            if rd == 0:
+                ring(k)
+
+        sync("g", ["x%d" % rd], [])
+        if rel:
+            put(rel[0], u8(T[pq][:, 0:HALF]), u8(T[xq][:, 0:HALF]), RX)
+            put(rel[1], u8(T[pq][:, HALF:C]), u8(T[xq][:, HALF:C]), RX)
+            put(rel[0], T[pks][:], T[xs][:], RX)
+        else:
+            put(dst, u8(T[pq][:]), u8(T[xq][:]), RX)
+            put(dst, T[pks][:], T[xs][:], RX)
+        listto = rel[1] if rel else dst
+        if backrel:
+            wr["p%d" % rd] = (RX, 2 * width(backrel[0], core) + width(backrel[1], core), {})
+            nl = width(backrel[1], core)
+        else:
+            wr["p%d" % rd] = (RX, 2 * width(dst, core), {})
+            nl = width(dst, core)
+        wr["livp%d" % rd] = (RI, nl, {RI: nl})
+        wr["lbp%d" % rd] = (RB, nl, {RB: nl})
+        wr["lep%d" % rd] = (RE, nl, {RE: nl})
+        wr["p%d" % rd][2][RX] = wr["p%d" % rd][1]
+
+        mm(0, "urq", "ursc", 0, xq, xs, ["urq", "ursc", "x%d" % rd])
+        ts(T.pp[:], bank(0), 0.0, GT, ["b0"], ["pp"])
+        cp(T.r1[:], T.pp[:].indirect(lst("iv%d" % rd)), ["pp", "liv%d" % rd], ["r1"], "s")
+        cp(T.r2[:], T.pp[:].indirect(lst("mi")), ["pp", "lmi"], ["r2"])
+        c2, e2 = scan(T.r2[:], C, "r2")
+        c1, e1 = scan(T.r1[:], C, "r1")
+        tt(T.t1[:], e1, e2, ADD, [c1, c2], ["t1"])
+        ts(T.bo[:], T.t1[:], T.thr[:, 0:1], GE, ["t1", "thr"], ["bo"])
+        tt(T.td[:], T.bo[:], T.ndw[:], MUL, ["bo", "ndw"], ["td"])
+        tt(T.tw[:], T.td[:], T.nim[:, 0:KW], ADD, ["td", "nim"], ["tw"])
+        cp(lst("wino"), T.tw[:], ["tw"], ["lwino"])
+        cp(T.win[:, 0:C], T.iota[:, 0:C + 2].indirect(lst("wino")), ["iota", "lwino"], ["win"], "s")
+        ts(lst("off1"), T.tw[:], float(C), MIN, ["tw"], ["loff1"])
+        imo, imn = "im%d" % (rd % 2), "im%d" % ((rd + 1) % 2)
+        tt(T.di2[:], T.bo[:], T.diw[:], MUL, ["bo", "diw"], ["di2"])
+        tt(T[imn][:, 0:KW], T.di2[:], T[imo][:, 0:KW], ADD, ["di2", imo], [imn])
+        cp(lst("iv%d" % (rd + 1)), T[imn][:, 0:KW], [imn], ["liv%d" % (rd + 1)])
+        sync("g", ["liv%d" % (rd + 1)], [])
+        put(listto, T["livp%d" % rd][:], T["liv%d" % (rd + 1)][:], RI)
+        if rd == 0:
+            for b in range(4):
+                op("v", lambda e: e.quantize_mx(T.eq[:, 128 * b:128 * b + 128], T.esc[:, 128 * b:128 * b + 128],
+                                                T.et[:, 3 - b:515 - b]), ["et"], ["e%d" % b])
+        for b in range(4):
+            mm(1 + b, "eq", "esc", 128 * b, xq, xs, ["e%d" % b, "x%d" % rd])
+        extra(2)
+        if rd == 0:
+            cp(T.uda[:], T.iota[:, 0:C].indirect(lst("udi")), ["iota", "ludi"], ["uda"], "s")
+        cp(T.h1[:, 0:C], T.win[:, 0:C + 2].indirect(lst("off1")), ["win", "wine", "loff1"], ["h1"])
+        cp(T.r3[:], T.pp[:].indirect(lst("mto")), ["pp", "lmto"], ["r3"], "s")
+        for b in range(4):
+            cp(pl("th", b), bank(1 + b), ["b%d" % (1 + b)], ["th%d" % b], "s")
+        hs = ["h1", "h2", "h4", "h8"]
+        for i in range(4):
+            of = T.lhoff[:, i * KW:(i + 1) * KW]
+            wrap(T[hs[i]][:, 0:C], C, hs[i], of, "lhoff%d" % i)
+            extra(3 + i)
+            nx = hs[i + 1] if i < 3 else "hx"
+            cp(T[nx][:, 0:C], T[hs[i]][:, 0:C + 2].indirect(of), [hs[i], hs[i] + "e", "lhoff%d" % i], [nx])
+        c1, e1 = scan(T.hx[:], C, "hx")
+        tt(T.ff[:], e1, T.nbw[:], ADD, [c1, "nbw"], ["ff"])
+        cp(lst("foff"), T.ff[:], ["ff"], ["lfoff"])
+        extra(7)
+        for b in range(8, -1, -1):
+            cp(T.fl[:, 32 * b:32 * b + 32], T.fl[:, 32 * b + 32:C + 2].indirect(T.lfoff[:, 2 * b:2 * b + 2]), ["fl", "fle", "lfoff"], ["fl"])
+        extra(8)
+        if rd == 0:
+            ring_end()
+        def partner():
+            for b in range(4):
+                k = (5, 6, 7, 0)[b]
+                mm(k, "eq", "esc", 128 * b, pq, pks, ["e%d" % b, "p%d" % rd])
+                cp(pl("tp", b), bank(k), ["b%d" % k], ["tp%d" % b], "s")
+
+        if rd in EARLY:
+            partner()
+        op("s", lambda e: e.activation(T.nf[:], T.fl[:, 0:C].indirect(lst("ordo")), IDENT, bias=1.0, scale=-1.0), ["fl", "lordo"], ["nf"])
+        tt(T.fo[:], T.fl[:, 0:C].indirect(lst("ordo")), T.oo[:], MUL, ["fl", "lordo", "oo"], ["fo"])
+        op("v", lambda e: e.tensor_tensor_scan(T.sa[:], T.nf[:], T.fo[:], 0.0, MUL, ADD), ["nf", "fo"], ["sa"])
+        op("v", lambda e: e.tensor_tensor_scan(T.sb[:], T.nf[:], T.fo[:], T.sa[:, C - 1:C], MUL, ADD), ["nf", "fo", "sa"], ["sb"])
+        cp(T.br[:], T.sb[:].indirect(lst("poso")), ["sb", "lposo"], ["br"])
+        wrap(T.br[:], C, "br", lst("bo%d" % rd), "lbo%d" % rd)
+        sync("g", ["lbo%d" % rd], [])
+        put(listto, T["lbp%d" % rd][:], T["lbo%d" % rd][:], RB)
+        if rd not in EARLY:
+            partner()
+        for b in range(4):
+            cp(pl("gv", b), pl("tp", b).indirect(lst("ivp%d" % rd)), ["tp%d" % b, "livp%d" % rd], ["gv%d" % b], "s")
+        c1, e1 = scan(T.pp[:], C, "pp")
+        c2, e2 = scan(T.r3[:], C, "r3")
+        tt(T.t3[:], e1, e2, ADD, [c1, c2], ["t3"])
+        ts(T.bj[:], T.t3[:], T.thr[:, 0:1], GE, ["t3", "thr"], ["bj"])
+        tt(T.dj[:], T.bj[:], T.dtw[:], MUL, ["bj", "dtw"], ["dj"])
+        tt(T.tf[:], T.dj[:], JW, ADD, ["dj"] + JK, ["tf"])
+        cp(lst("tauo"), T.tf[:], ["tf"], ["ltauo"])
+        uo, un = ud[rd % 2], ud[(rd + 1) % 2]
+        cp(T[un][:], T[uo][:].indirect(lst("tauo")), [uo, "ltauo"], [un], "s")
+        cp(T.r2[:], T.br[:].indirect(lst("ivp%d" % rd)), ["br", "livp%d" % rd], ["r2"])
+        wrap(T.r2[:], C, "r2", lst("eo%d" % rd), "leo%d" % rd)
+        sync("g", ["leo%d" % rd], [])
+        put(listto, T["lep%d" % rd][:], T["leo%d" % rd][:], RE)
+        wrap(T[un][:], C, un, lst("udo"), "ludo")
+        for b in range(4):
+            cp(pl("tu", b), pl("th", b).indirect(lst("udo")), ["th%d" % b, "ludo"], ["tu%d" % b], "s")
+        if rd < 2:
+            cp(T.mr[:], T.mtr[:].indirect(lst("iv%d" % (rd + 1))), ["mtr", "liv%d" % (rd + 1)], ["mr"], "s")
+        for b in range(4):
+            tt(T.zt[:, b:4 * C:4], pl("tp", b).indirect(lst("bp%d" % rd)), pl("gv", b), ADD,
+               ["tp%d" % b, "gv%d" % b, "lbp%d" % rd], ["zt%d" % b])
+        op("v", lambda e: e.quantize_mx(T.zq[:], T.zsc[:], T.zt[:]), ["zt%d" % b for b in range(4)], ["z"])
+        for b in range(4):
+            mm(1 + b, "wq", "wsc", 128 * b, "zq", "zsc", ["wq", "wsc", "z"])
+        for b in range(4):
+            op("s", lambda e: e.activation(pl("hh", b), bank(1 + b), COPY, scale=0.015625), ["b%d" % (1 + b)], ["hh%d" % b])
+        if rd < 2:
+            prepare(rd + 1)
+        else:
+            op("s", lambda e: e.activation(T.udf[:], T[un][:], COPY, bias=float(MID)), [un], ["udf"])
+            dma("y", T.uo[:], T.udf[0:128:16, :], ["udf"], [])
+            op("v", lambda e: e.quantize_mx(T.vq[:], T.vsc[:], T.vt[:]), ["vt"], ["v"])
+        for b in range(4):
+            tt(T.xt[:, b:4 * C:4], pl("hh", b).indirect(lst("ep%d" % rd)), pl("tu", b), ADD,
+               ["hh%d" % b, "tu%d" % b, "lep%d" % rd], ["xt%d" % b])
+        nq = rd + 1
+        op("v", lambda e: e.quantize_mx(T["x%dq" % nq][:], T["x%dsc" % nq][:], T.xt[:]), ["xt%d" % b for b in range(4)], ["x%d" % nq])
+
+    dma("y", T.oc[:], u8(T.x3q[:]), ["x3"], [])
+    for k in range(4):
+        dma("s" if k % 2 else "y", T.osc[4 * k:4 * k + 4, :], T.x3sc[32 * k:32 * k + 4, :], ["x3"], [])
+    mm(5, "vq", "vsc", 0, "x3q", "x3sc", ["v", "x3"])
+    cp(T.yf[:], bank(5), ["b5"], ["yf"])
+    dma("s", T.y[:], T.yf[:], ["yf"], [])
+    for s in dsems:
+        Q["y"].wait_ge(T.sem[s], 16)
+    for q in ("v", "s", "t", "g"):
+        g.wait_ge(T.sem[SEM[q]], cnt[q])
+    g.wait_ge(T.sem.snt, sent[0])

@@ -6,6 +6,7 @@ MID = 145
 BIG = 512.0
 SCAN = "float16"
 EARLY = (0, 1)
+CUT = 10
 
 SCRATCH = {}
 for _n in ("xin", "xt", "zt", "th", "tp", "tu", "gv", "hh"):
@@ -19,7 +20,7 @@ for _n, _w in (("x0", C), ("x1", C), ("x2", C), ("x3", C), ("p0", C), ("p1", C),
     SCRATCH[_n + "sc"] = ("sbuf", [128, _w], "uint8")
 for _n in ("iota", "win", "h1", "h2", "h4", "h8", "fl"):
     SCRATCH[_n] = ("sbuf", [128, 304], "bfloat16")
-for _n in ("iom", "pat", "pp", "r1", "r2", "r3", "hx", "nf", "fo", "sa", "sb", "br", "uda", "udb", "mtr", "mr", "oo"):
+for _n in ("iom", "pat", "patf", "pp", "r1", "r2", "r3", "hx", "nf", "fo", "sa", "sb", "br", "uda", "udb", "mtr", "mr", "oo"):
     SCRATCH[_n] = ("sbuf", [128, C], "bfloat16")
 SCRATCH["hpr"] = ("sbuf", [128, 9 * C], "bfloat16")
 for _n in ("c0", "c1", "c2", "c3"):
@@ -30,9 +31,9 @@ for _n in ("ivl", "mtl", "udl", "hpl"):
 SCRATCH["qi"] = ("sbuf", [128, 8], "int32")
 for _n in ("corr", "thr", "qz"):
     SCRATCH[_n] = ("sbuf", [128, 8], "float32")
-for _n in ("k16", "kb", "jw", "nbw", "mtw", "dtw", "t1", "bo", "td", "tw", "t3", "bj", "dj", "tf", "diw", "ndw", "ff", "di2"):
+for _n in ("k16", "kb", "jw", "mtw", "dtw", "t1", "t3", "bj", "dj", "tf", "diw", "di2"):
     SCRATCH[_n] = ("sbuf", [128, KW], "float32")
-for _n in ("jw2", "im0", "im1", "ta", "tb", "nim"):
+for _n in ("jw2", "im0", "im1", "ta", "tb", "nim", "fm0", "fm1", "fmo"):
     SCRATCH[_n] = ("sbuf", [128, 2 * KW], "float32")
 LOCAL = ("iv0", "mi", "mto", "udo", "wino", "off1", "poso", "tauo", "udi")
 SCRATCH["lloc"] = ("sbuf", [128, len(LOCAL) * KW], "uint16")
@@ -51,7 +52,7 @@ SEMAPHORES += ["%s%d" % (a, i) for a in ("rx", "ri", "rb", "re") for i in range(
 
 MUL, ADD, SUB, MAX, MIN = AluOpType.mult, AluOpType.add, AluOpType.subtract, AluOpType.max, AluOpType.min
 GT, GE, EQ = AluOpType.is_gt, AluOpType.is_ge, AluOpType.is_equal
-COPY, IDENT = ActivationFunctionType.Copy, ActivationFunctionType.Identity
+COPY, IDENT, SIGN = ActivationFunctionType.Copy, ActivationFunctionType.Identity, ActivationFunctionType.Sign
 
 
 def relays(topo, src, dst):
@@ -171,23 +172,29 @@ def rank_program(g, core, T, topo):
         else:
             op("s", lambda e: e.activation(out, in_, COPY), reads, writes)
 
+    def pick(out, win, off, reads, key, k=CUT):
+        if k < KW:
+            op("s", lambda e: e.activation(T[out][:, 16 * k:C], win.indirect(off(k, KW)), COPY), reads, [key + "s"])
+        op("v", lambda e: e.tensor_copy(T[out][:, 0:16 * k], win.indirect(off(0, k))), reads, [key])
+
     rot = [0]
 
-    def scan(row, n, key):
+    def scan(row, n, key, pat="pat"):
         b = "c%d" % (rot[0] % 4)
         rot[0] += 1
-        op("v", lambda e: e.tensor_tensor_scan(T[b][:, 0:n], row, T.pat[:, 0:n], -2 * BIG, MAX, ADD), [key, "pat"], [b])
+        op("v", lambda e: e.tensor_tensor_scan(T[b][:, 0:n], row, T[pat][:, 0:n], -2 * BIG, MAX, ADD),
+           [key, key + "s", pat], [b])
         return b, T[b][:, 15:n:16]
 
     def wrap(row, n, key, off, okey):
         b, e = scan(row, n, key)
         ts(off, e, T.corr[:, 0:1], ADD, [b, "corr"], [okey])
 
-    def lst(name):
+    def lst(name, a=0, b=KW):
         if name in LOCAL:
             o = KW * LOCAL.index(name)
-            return T.lloc[:, o:o + KW]
-        return T["l" + name][:, 0:KW]
+            return T.lloc[:, o + a:o + b]
+        return T["l" + name][:, a:b]
 
     dma("s", T.hpl[:], T.hp[:], [], ["hpl"])
     dma("y", T.xin[:], T.x[:], [], ["xin"])
@@ -199,7 +206,7 @@ def rank_program(g, core, T, topo):
     dma("y", T.wsc[:], T.ws[:], [], ["wsc"])
     dma("y", T.vt[:], T.v[:], [], ["vt"])
 
-    op("v", lambda e: e.memset(T.lordo[:], 0), [], ["lordo"])
+    op("v", lambda e: e.memset(T.lordo[:], C - 1), [], ["lordo"])
     op("v", lambda e: e.memset(T.oo[:], float(-MID)), [], ["oo"])
     op("g", lambda e: e.iota(T.qi[:], [[0, 8]], 0, 1), [], ["qi"])
     op("g", lambda e: e.iota(T.pati[:], [[1, C]], 1024, -1), [], ["pati"])
@@ -225,13 +232,19 @@ def rank_program(g, core, T, topo):
     cp(T.jw[:, 0:1], T.qi[:, 0:1], ["qi"], ["jwq"])
     ts(T.jw2[:, 0:KW], T.k16[:], T.jw[:, 0:1], ADD, ["k16", "jwq"], ["jwa"])
     ts(T.jw2[:, KW:2 * KW], T.k16[:], T.jw[:, 0:1], ADD, ["k16", "jwq"], ["jwb"])
-    ts(T.nbw[:], T.kb[:], T.corr[:, 0:1], ADD, ["kb", "corr"], ["nbw"])
     JW = T.jw2[:, 0:KW]
     JK = ["jwa", "jwb"]
 
     def ring(k):
         a, b = (16, 18) if k < 6 or k == 8 else (14, 18) if k == 6 else (10, 18)
         o = 0 if k == 8 else 16 * a - (1 << k)
+        if k == 0:
+            cp(T.oo[:, 256:C], T.hpr[:, 0:C].indirect(T.lordo[:, a:b]), ["hpr0", "lordo"], ["oo"], "s")
+            cp(T.hpr[:, C:2 * C], T.hpr[:, 0:C].indirect(T.lhp[:, 0:KW]), ["hpr0", "lhp0"], ["hpr1"], "s")
+            cp(T.oo[:, 255:C - 1], T.hpr[:, C:2 * C].indirect(T.lordo[:, a:b]), ["hpr1", "lordo", "oo"], ["oo"], "s")
+            wrap(T.hpr[:, C:2 * C], C, "hpr1", T.lhp[:, KW:2 * KW], "lhp1")
+            wrap(T.oo[:, 256:C], 32, "oo", T.lordo[:, 16:18], "lordo")
+            return
         cp(T.oo[:, o:o + 16 * (b - a)], T.hpr[:, k * C:(k + 1) * C].indirect(T.lordo[:, a:b]), ["hpr%d" % k, "lordo"], ["oo"], "s")
         if k < 8:
             cp(T.hpr[:, (k + 1) * C:(k + 2) * C], T.hpr[:, k * C:(k + 1) * C].indirect(T.lhp[:, k * KW:(k + 1) * KW]),
@@ -262,11 +275,14 @@ def rank_program(g, core, T, topo):
         ts(T.tb[:], T[im][:], float(C + 1), SUB, [im, im + "m"], ["tb"])
         tt(T.diw[:], T[im][:, KW:2 * KW], T[im][:, 0:KW], SUB, [im, im + "m"], ["diw"])
         tt(T.nim[:], T.ta[:], T.tb[:], MUL, ["ta", "tb"], ["nim"])
-        tt(T.ndw[:], T.nim[:, KW:2 * KW], T.nim[:, 0:KW], SUB, ["nim"], ["ndw"])
-        ts(T.nim[:], T.nim[:], float(C + 1), ADD, ["nim"], ["nim"])
+        tt(T.fm0[:, 1:2 * KW:2], T.nim[:, KW:2 * KW], T.nim[:, 0:KW], SUB, ["nim"], ["fm0"])
+        ts(T.fm1[:, 1:2 * KW:2], T.nim[:, 0:KW], float(C + 1), ADD, ["nim"], ["fm1"])
 
     for b in ("win", "h1", "h2", "h4", "h8"):
         cp(T[b][:, C:C + 2], T.iota[:, C:C + 2], ["iota"], [b + "e"])
+    op("v", lambda e: e.memset(T.fm0[:], 0.0), [], ["fm0"])
+    cp(T.patf[:], T.pat[:], ["pat"], ["patf"])
+    tt(T.patf[:, 15:C:16], T.pat[:, 15:C:16], T.kb[:], ADD, ["pat", "kb", "patf"], ["patf"])
     op("v", lambda e: e.memset(T.fl[:, C + 1:C + 2], 0.0), [], ["fle"])
     op("v", lambda e: e.memset(T.fl[:, C:C + 1], 1.0), [], ["fl"])
     op("v", lambda e: e.memset(T.iom[:, 0:1], float(C - 1 - MID)), ["iom"], ["iom"])
@@ -279,9 +295,9 @@ def rank_program(g, core, T, topo):
        ["u", "luo"], ["urq"])
     op("s", lambda e: e.activation(T.ursc[:, 0:128], T.usc[:, 0:128].indirect(T.luo[:, 0:8]), COPY), ["u", "luo"], ["ursc"])
 
-    def mm(bank, l, ls, a, r, rs, reads):
-        op("t", lambda e: e.matmul_mx(T.ps[:, 512 * bank:512 * bank + C], T[l][:, a:a + 128], T[ls][:, a:a + 128], T[r][:, 0:C],
-                                      T[rs][:, 0:C], True, True), reads, ["b%d" % bank])
+    def mm(bank, l, ls, a, r, rs, reads, c=0, d=C):
+        op("t", lambda e: e.matmul_mx(T.ps[:, 512 * bank:512 * bank + d - c], T[l][:, a:a + 128], T[ls][:, a:a + 128], T[r][:, c:d],
+                                      T[rs][:, c:d], True, True), reads, ["b%d" % bank])
 
     def bank(k):
         return T.ps[:, 512 * k:512 * k + C]
@@ -322,21 +338,25 @@ def rank_program(g, core, T, topo):
         wr["lep%d" % rd] = (RE, nl, {RE: nl})
         wr["p%d" % rd][2][RX] = wr["p%d" % rd][1]
 
-        mm(0, "urq", "ursc", 0, xq, xs, ["urq", "ursc", "x%d" % rd])
-        ts(T.pp[:], bank(0), 0.0, GT, ["b0"], ["pp"])
-        cp(T.r1[:], T.pp[:].indirect(lst("iv%d" % rd)), ["pp", "liv%d" % rd], ["r1"], "s")
-        cp(T.r2[:], T.pp[:].indirect(lst("mi")), ["pp", "lmi"], ["r2"])
+        mm(0, "urq", "ursc", 0, xq, xs, ["urq", "ursc", "x%d" % rd], 0, HALF)
+        mm(5, "urq", "ursc", 0, xq, xs, ["urq", "ursc", "x%d" % rd], HALF, C)
+        ts(T.pp[:, 0:HALF], T.ps[:, 0:HALF], 0.0, GT, ["b0"], ["pp"])
+        op("s", lambda e: e.activation(T.pp[:, HALF:C], T.ps[:, 2560:2560 + HALF], SIGN), ["b5"], ["pps"])
+        cp(T.r1[:], T.pp[:].indirect(lst("iv%d" % rd)), ["pp", "pps", "liv%d" % rd], ["r1"], "s")
+        cp(T.r3[:], T.pp[:].indirect(lst("mto")), ["pp", "pps", "lmto"], ["r3"], "s")
+        cp(T.r2[:], T.pp[:].indirect(lst("mi")), ["pp", "pps", "lmi"], ["r2"])
         c2, e2 = scan(T.r2[:], C, "r2")
         c1, e1 = scan(T.r1[:], C, "r1")
         tt(T.t1[:], e1, e2, ADD, [c1, c2], ["t1"])
-        ts(T.bo[:], T.t1[:], T.thr[:, 0:1], GE, ["t1", "thr"], ["bo"])
-        tt(T.td[:], T.bo[:], T.ndw[:], MUL, ["bo", "ndw"], ["td"])
-        tt(T.tw[:], T.td[:], T.nim[:, 0:KW], ADD, ["td", "nim"], ["tw"])
-        cp(lst("wino"), T.tw[:], ["tw"], ["lwino"])
-        cp(T.win[:, 0:C], T.iota[:, 0:C + 2].indirect(lst("wino")), ["iota", "lwino"], ["win"], "s")
-        ts(lst("off1"), T.tw[:], float(C), MIN, ["tw"], ["loff1"])
+        ts(T.fm1[:, 0:2 * KW:2], T.t1[:], T.thr[:, 0:1], GE, ["t1", "thr"], ["bo"])
+        op("v", lambda e: e.tensor_tensor_scan(T.fmo[:], T.fm0[:], T.fm1[:], 0.0, MUL, ADD), ["bo", "fm0", "fm1"], ["fmo"])
+        tw = T.fmo[:, 1:2 * KW:2]
+        cp(lst("wino"), tw, ["fmo"], ["lwino"])
+        op("s", lambda e: e.activation(T.win[:, 96:C], T.iota[:, 0:C + 2].indirect(lst("wino", 6, KW)), COPY), ["iota", "lwino"], ["wins"])
+        ts(lst("off1"), tw, float(C), MIN, ["fmo"], ["loff1"])
+        cp(T.win[:, 0:96], T.iota[:, 0:C + 2].indirect(lst("wino", 0, 6)), ["iota", "lwino"], ["win"])
         imo, imn = "im%d" % (rd % 2), "im%d" % ((rd + 1) % 2)
-        tt(T.di2[:], T.bo[:], T.diw[:], MUL, ["bo", "diw"], ["di2"])
+        tt(T.di2[:], T.fm1[:, 0:2 * KW:2], T.diw[:], MUL, ["bo", "diw"], ["di2"])
         tt(T[imn][:, 0:KW], T.di2[:], T[imo][:, 0:KW], ADD, ["di2", imo], [imn])
         cp(lst("iv%d" % (rd + 1)), T[imn][:, 0:KW], [imn], ["liv%d" % (rd + 1)])
         sync("g", ["liv%d" % (rd + 1)], [])
@@ -347,23 +367,22 @@ def rank_program(g, core, T, topo):
                                                 T.et[:, 3 - b:515 - b]), ["et"], ["e%d" % b])
         for b in range(4):
             mm(1 + b, "eq", "esc", 128 * b, xq, xs, ["e%d" % b, "x%d" % rd])
+        cut = CUT if rd else KW
         extra(2)
         if rd == 0:
             cp(T.uda[:], T.iota[:, 0:C].indirect(lst("udi")), ["iota", "ludi"], ["uda"], "s")
-        cp(T.h1[:, 0:C], T.win[:, 0:C + 2].indirect(lst("off1")), ["win", "wine", "loff1"], ["h1"])
-        cp(T.r3[:], T.pp[:].indirect(lst("mto")), ["pp", "lmto"], ["r3"], "s")
-        for b in range(4):
-            cp(pl("th", b), bank(1 + b), ["b%d" % (1 + b)], ["th%d" % b], "s")
+        pick("h1", T.win[:, 0:C + 2], lambda a, b: lst("off1", a, b), ["win", "wins", "wine", "loff1"], "h1", cut)
         hs = ["h1", "h2", "h4", "h8"]
         for i in range(4):
             of = T.lhoff[:, i * KW:(i + 1) * KW]
             wrap(T[hs[i]][:, 0:C], C, hs[i], of, "lhoff%d" % i)
             extra(3 + i)
+            cp(pl("th", i), bank(1 + i), ["b%d" % (1 + i)], ["th%d" % i], "s")
             nx = hs[i + 1] if i < 3 else "hx"
-            cp(T[nx][:, 0:C], T[hs[i]][:, 0:C + 2].indirect(of), [hs[i], hs[i] + "e", "lhoff%d" % i], [nx])
-        c1, e1 = scan(T.hx[:], C, "hx")
-        tt(T.ff[:], e1, T.nbw[:], ADD, [c1, "nbw"], ["ff"])
-        cp(lst("foff"), T.ff[:], ["ff"], ["lfoff"])
+            pick(nx, T[hs[i]][:, 0:C + 2], lambda a, b: T.lhoff[:, i * KW + a:i * KW + b],
+                 [hs[i], hs[i] + "s", hs[i] + "e", "lhoff%d" % i], nx, cut)
+        c1, e1 = scan(T.hx[:], C, "hx", "patf")
+        ts(lst("foff"), e1, T.corr[:, 0:1], ADD, [c1, "corr"], ["lfoff"])
         extra(7)
         for b in range(8, -1, -1):
             cp(T.fl[:, 32 * b:32 * b + 32], T.fl[:, 32 * b + 32:C + 2].indirect(T.lfoff[:, 2 * b:2 * b + 2]), ["fl", "fle", "lfoff"], ["fl"])
@@ -380,16 +399,18 @@ def rank_program(g, core, T, topo):
             partner()
         op("s", lambda e: e.activation(T.nf[:], T.fl[:, 0:C].indirect(lst("ordo")), IDENT, bias=1.0, scale=-1.0), ["fl", "lordo"], ["nf"])
         tt(T.fo[:], T.fl[:, 0:C].indirect(lst("ordo")), T.oo[:], MUL, ["fl", "lordo", "oo"], ["fo"])
-        op("v", lambda e: e.tensor_tensor_scan(T.sa[:], T.nf[:], T.fo[:], 0.0, MUL, ADD), ["nf", "fo"], ["sa"])
-        op("v", lambda e: e.tensor_tensor_scan(T.sb[:], T.nf[:], T.fo[:], T.sa[:, C - 1:C], MUL, ADD), ["nf", "fo", "sa"], ["sb"])
-        cp(T.br[:], T.sb[:].indirect(lst("poso")), ["sb", "lposo"], ["br"])
+        op("v", lambda e: e.tensor_tensor_scan(T.sb[:], T.nf[:], T.fo[:], 0.0, MUL, ADD), ["nf", "fo"], ["sb"])
+        pick("br", T.sb[:], lambda a, b: lst("poso", a, b), ["sb", "lposo"], "br")
         wrap(T.br[:], C, "br", lst("bo%d" % rd), "lbo%d" % rd)
         sync("g", ["lbo%d" % rd], [])
         put(listto, T["lbp%d" % rd][:], T["lbo%d" % rd][:], RB)
         if rd not in EARLY:
             partner()
-        for b in range(4):
+        def past(b):
             cp(pl("gv", b), pl("tp", b).indirect(lst("ivp%d" % rd)), ["tp%d" % b, "livp%d" % rd], ["gv%d" % b], "s")
+
+        past(0)
+        past(1)
         c1, e1 = scan(T.pp[:], C, "pp")
         c2, e2 = scan(T.r3[:], C, "r3")
         tt(T.t3[:], e1, e2, ADD, [c1, c2], ["t3"])
@@ -399,7 +420,9 @@ def rank_program(g, core, T, topo):
         cp(lst("tauo"), T.tf[:], ["tf"], ["ltauo"])
         uo, un = ud[rd % 2], ud[(rd + 1) % 2]
         cp(T[un][:], T[uo][:].indirect(lst("tauo")), [uo, "ltauo"], [un], "s")
-        cp(T.r2[:], T.br[:].indirect(lst("ivp%d" % rd)), ["br", "livp%d" % rd], ["r2"])
+        past(2)
+        past(3)
+        cp(T.r2[:], T.br[:].indirect(lst("ivp%d" % rd)), ["br", "brs", "livp%d" % rd], ["r2"])
         wrap(T.r2[:], C, "r2", lst("eo%d" % rd), "leo%d" % rd)
         sync("g", ["leo%d" % rd], [])
         put(listto, T["lep%d" % rd][:], T["leo%d" % rd][:], RE)

@@ -186,9 +186,13 @@ def rank_program(g, core, T, topo):
            [key, key + "s", pat], [b])
         return b, T[b][:, 15:n:16]
 
-    def wrap(row, n, key, off, okey):
-        b, e = scan(row, n, key)
-        ts(off, e, T.corr[:, 0:1], ADD, [b, "corr"], [okey])
+    def wraps(jobs):
+        es = [scan(j[0], j[1], j[2], j[5] if len(j) > 5 else "pat") for j in jobs]
+        for (b, e), j in zip(es, jobs):
+            ts(j[3], e, T.corr[:, 0:1], ADD, [b, "corr"], [j[4]])
+
+    def wrap(*job):
+        wraps([job])
 
     def lst(name, a=0, b=KW):
         if name in LOCAL:
@@ -197,17 +201,16 @@ def rank_program(g, core, T, topo):
         return T["l" + name][:, a:b]
 
     dma("s", T.hpl[:], T.hp[:], [], ["hpl"])
-    dma("y", T.xin[:], T.x[:], [], ["xin"])
+    dma("y", T.ut[:], T.u[:], [], ["ut"])
     dma("s", T.ivl[:], T.iv[:], [], ["ivl"])
     dma("s", T.mtl[:], T.mt[:], [], ["mtl"])
-    dma("y", T.ut[:], T.u[:], [], ["ut"])
+    dma("y", T.xin[:], T.x[:], [], ["xin"])
     dma("s", T.udl[:], T.ud[:], [], ["udl"])
     dma("y", u8(T.wq[:]), T.wc[:], [], ["wq"])
     dma("y", T.wsc[:], T.ws[:], [], ["wsc"])
     dma("y", T.vt[:], T.v[:], [], ["vt"])
 
     op("v", lambda e: e.memset(T.lordo[:], C - 1), [], ["lordo"])
-    op("v", lambda e: e.memset(T.oo[:], float(-MID)), [], ["oo"])
     op("g", lambda e: e.iota(T.qi[:], [[0, 8]], 0, 1), [], ["qi"])
     op("g", lambda e: e.iota(T.pati[:], [[1, C]], 1024, -1), [], ["pati"])
     op("g", lambda e: e.iota(T.iota[:], [[1, 304]], -MID, 0, allow_small_or_imprecise_dtypes=True), [], ["iota"])
@@ -223,9 +226,9 @@ def rank_program(g, core, T, topo):
     ts(T.pati[:], T.pati[:], 15, AluOpType.bitwise_and, ["pati"], ["pati"])
     ts(T.pat[:], T.pati[:], 0.0, EQ, ["pati"], ["pat"], BIG, MUL)
     ts(T.hx[:], T.pati[:], 15.0, EQ, ["pati"], ["hx"], -2 * BIG, MUL)
-    tt(T.pat[:], T.pat[:], T.hx[:], ADD, ["pat", "hx"], ["pat"])
     cp(T.lhp[:, 0:KW], T.hpl[:], ["hpl"], ["lhp0"])
     cp(T.hpr[:, 0:C], T.iota[:, 0:C].indirect(T.lhp[:, 0:KW]), ["iota", "lhp0"], ["hpr0"], "s")
+    tt(T.pat[:], T.pat[:], T.hx[:], ADD, ["pat", "hx"], ["pat"])
     cp(lst("iv0"), T.ivl[:], ["ivl"], ["liv0"])
     cp(lst("mto"), T.mtl[:], ["mtl"], ["lmto"])
     ts(T.thr[:], T.qz[:], -4 * BIG, MUL, ["qz"], ["thr"], 1.5 + 2 * BIG, ADD)
@@ -235,34 +238,42 @@ def rank_program(g, core, T, topo):
     JW = T.jw2[:, 0:KW]
     JK = ["jwa", "jwb"]
 
-    def ring(k):
+    def square(k):
+        if k < 8:
+            cp(T.hpr[:, (k + 1) * C:(k + 2) * C], T.hpr[:, k * C:(k + 1) * C].indirect(T.lhp[:, k * KW:(k + 1) * KW]),
+               ["hpr%d" % k, "lhp%d" % k], ["hpr%d" % (k + 1)], "s")
+
+    def places(k):
         a, b = (16, 18) if k < 6 or k == 8 else (14, 18) if k == 6 else (10, 18)
         o = 0 if k == 8 else 16 * a - (1 << k)
         if k == 0:
             cp(T.oo[:, 256:C], T.hpr[:, 0:C].indirect(T.lordo[:, a:b]), ["hpr0", "lordo"], ["oo"], "s")
-            cp(T.hpr[:, C:2 * C], T.hpr[:, 0:C].indirect(T.lhp[:, 0:KW]), ["hpr0", "lhp0"], ["hpr1"], "s")
             cp(T.oo[:, 255:C - 1], T.hpr[:, C:2 * C].indirect(T.lordo[:, a:b]), ["hpr1", "lordo", "oo"], ["oo"], "s")
-            wrap(T.hpr[:, C:2 * C], C, "hpr1", T.lhp[:, KW:2 * KW], "lhp1")
-            wrap(T.oo[:, 256:C], 32, "oo", T.lordo[:, 16:18], "lordo")
-            return
-        cp(T.oo[:, o:o + 16 * (b - a)], T.hpr[:, k * C:(k + 1) * C].indirect(T.lordo[:, a:b]), ["hpr%d" % k, "lordo"], ["oo"], "s")
-        if k < 8:
-            cp(T.hpr[:, (k + 1) * C:(k + 2) * C], T.hpr[:, k * C:(k + 1) * C].indirect(T.lhp[:, k * KW:(k + 1) * KW]),
-               ["hpr%d" % k, "lhp%d" % k], ["hpr%d" % (k + 1)], "s")
-        s0, s1 = (256, 288) if k < 5 else (o, o + 16 * (b - a))
-        wrap(T.oo[:, s0:s1], s1 - s0, "oo", T.lordo[:, s0 // 16:s1 // 16], "lordo")
+        else:
+            cp(T.oo[:, o:o + 16 * (b - a)], T.hpr[:, k * C:(k + 1) * C].indirect(T.lordo[:, a:b]), ["hpr%d" % k, "lordo"], ["oo"], "s")
+        return (256, 288) if k < 5 else (o, o + 16 * (b - a))
+
+    def ring(k, jobs=()):
+        jobs = list(jobs)
+        square(k)
+        s0, s1 = places(k)
         if k < 7:
-            wrap(T.hpr[:, (k + 1) * C:(k + 2) * C], C, "hpr%d" % (k + 1), T.lhp[:, (k + 1) * KW:(k + 2) * KW], "lhp%d" % (k + 1))
+            jobs.append((T.hpr[:, (k + 1) * C:(k + 2) * C], C, "hpr%d" % (k + 1), T.lhp[:, (k + 1) * KW:(k + 2) * KW],
+                         "lhp%d" % (k + 1)))
+        jobs.append((T.oo[:, s0:s1], s1 - s0, "oo", T.lordo[:, s0 // 16:s1 // 16], "lordo"))
+        wraps(jobs)
 
-    def ring_end():
-        cp(T.r1[:, 0:C].indirect(T.lordo[:, 0:KW]), T.iom[:], ["iom", "lordo"], ["r1"])
-        wrap(T.r1[:], C, "r1", lst("poso"), "lposo")
-
+    op("v", lambda e: e.tensor_copy(T.luo[:], T.uoi[:]), ["uoi"], ["luo"])
+    op("v", lambda e: e.memset(T.fm0[:], 0.0), [], ["fm0"])
+    op("v", lambda e: e.memset(T.fl[:, C + 1:C + 2], 0.0), [], ["fle"])
+    op("v", lambda e: e.memset(T.fl[:, C:C + 1], 1.0), [], ["fl"])
+    cp(T.patf[:], T.pat[:], ["pat"], ["patf"])
+    tt(T.patf[:, 15:C:16], T.pat[:, 15:C:16], T.kb[:], ADD, ["pat", "kb", "patf"], ["patf"])
+    cp(T.im0[:, 0:KW], T.ivl[:], ["ivl"], ["im0"])
+    cp(T.mtw[:], T.mtl[:], ["mtl"], ["mtw"])
     ring(0)
     cp(T.mtr[:], T.iota[:, 0:C].indirect(lst("mto")), ["iota", "lmto"], ["mtr"], "s")
     cp(T.mr[:], T.mtr[:].indirect(lst("iv0")), ["mtr", "liv0"], ["mr"], "s")
-    cp(T.im0[:, 0:KW], T.ivl[:], ["ivl"], ["im0"])
-    cp(T.mtw[:], T.mtl[:], ["mtl"], ["mtw"])
     tt(T.dtw[:], T.mtw[:], JW, SUB, ["mtw"] + JK, ["dtw"])
     cp(lst("udi"), T.udl[:], ["udl"], ["ludi"])
 
@@ -280,20 +291,14 @@ def rank_program(g, core, T, topo):
 
     for b in ("win", "h1", "h2", "h4", "h8"):
         cp(T[b][:, C:C + 2], T.iota[:, C:C + 2], ["iota"], [b + "e"])
-    op("v", lambda e: e.memset(T.fm0[:], 0.0), [], ["fm0"])
-    cp(T.patf[:], T.pat[:], ["pat"], ["patf"])
-    tt(T.patf[:, 15:C:16], T.pat[:, 15:C:16], T.kb[:], ADD, ["pat", "kb", "patf"], ["patf"])
-    op("v", lambda e: e.memset(T.fl[:, C + 1:C + 2], 0.0), [], ["fle"])
-    op("v", lambda e: e.memset(T.fl[:, C:C + 1], 1.0), [], ["fl"])
     op("v", lambda e: e.memset(T.iom[:, 0:1], float(C - 1 - MID)), ["iom"], ["iom"])
-    prepare(0)
-    op("v", lambda e: e.tensor_copy(T.luo[:], T.uoi[:]), ["uoi"], ["luo"])
-    op("v", lambda e: e.quantize_mx(T.x0q[:], T.x0sc[:], T.xin[:]), ["xin"], ["x0"])
-    ring(1)
     op("v", lambda e: e.quantize_mx(T.uq[:], T.usc[:], T.ut[:]), ["ut"], ["u"])
     op("v", lambda e: e.tensor_copy(T.urq[:, 0:128].bitcast(dt.uint32), T.uq[:, 0:128].bitcast(dt.uint32).indirect(T.luo[:, 0:8])),
        ["u", "luo"], ["urq"])
     op("s", lambda e: e.activation(T.ursc[:, 0:128], T.usc[:, 0:128].indirect(T.luo[:, 0:8]), COPY), ["u", "luo"], ["ursc"])
+    prepare(0)
+    op("v", lambda e: e.quantize_mx(T.x0q[:], T.x0sc[:], T.xin[:]), ["xin"], ["x0"])
+    ring(1)
 
     def mm(bank, l, ls, a, r, rs, reads, c=0, d=C):
         op("t", lambda e: e.matmul_mx(T.ps[:, 512 * bank:512 * bank + d - c], T[l][:, a:a + 128], T[ls][:, a:a + 128], T[r][:, c:d],
@@ -304,6 +309,10 @@ def rank_program(g, core, T, topo):
 
     def pl(name, b):
         return T[name][:, b * C:(b + 1) * C]
+
+    def constants(b):
+        op("v", lambda e: e.quantize_mx(T.eq[:, 128 * b:128 * b + 128], T.esc[:, 128 * b:128 * b + 128], T.et[:, 3 - b:515 - b]),
+           ["et"], ["e%d" % b])
 
     ud = ["uda", "udb"]
     for rd, step in enumerate(STEP):
@@ -341,6 +350,9 @@ def rank_program(g, core, T, topo):
         mm(0, "urq", "ursc", 0, xq, xs, ["urq", "ursc", "x%d" % rd], 0, HALF)
         mm(5, "urq", "ursc", 0, xq, xs, ["urq", "ursc", "x%d" % rd], HALF, C)
         ts(T.pp[:, 0:HALF], T.ps[:, 0:HALF], 0.0, GT, ["b0"], ["pp"])
+        if rd == 0:
+            constants(0)
+            constants(1)
         op("s", lambda e: e.activation(T.pp[:, HALF:C], T.ps[:, 2560:2560 + HALF], SIGN), ["b5"], ["pps"])
         cp(T.r1[:], T.pp[:].indirect(lst("iv%d" % rd)), ["pp", "pps", "liv%d" % rd], ["r1"], "s")
         cp(T.r3[:], T.pp[:].indirect(lst("mto")), ["pp", "pps", "lmto"], ["r3"], "s")
@@ -362,9 +374,8 @@ def rank_program(g, core, T, topo):
         sync("g", ["liv%d" % (rd + 1)], [])
         put(listto, T["livp%d" % rd][:], T["liv%d" % (rd + 1)][:], RI)
         if rd == 0:
-            for b in range(4):
-                op("v", lambda e: e.quantize_mx(T.eq[:, 128 * b:128 * b + 128], T.esc[:, 128 * b:128 * b + 128],
-                                                T.et[:, 3 - b:515 - b]), ["et"], ["e%d" % b])
+            constants(2)
+            constants(3)
         for b in range(4):
             mm(1 + b, "eq", "esc", 128 * b, xq, xs, ["e%d" % b, "x%d" % rd])
         cut = CUT if rd else KW
@@ -375,20 +386,33 @@ def rank_program(g, core, T, topo):
         hs = ["h1", "h2", "h4", "h8"]
         for i in range(4):
             of = T.lhoff[:, i * KW:(i + 1) * KW]
-            wrap(T[hs[i]][:, 0:C], C, hs[i], of, "lhoff%d" % i)
-            extra(3 + i)
+            job = (T[hs[i]][:, 0:C], C, hs[i], of, "lhoff%d" % i)
+            if rd == 0:
+                ring(3 + i, [job])
+            else:
+                wraps([job])
             cp(pl("th", i), bank(1 + i), ["b%d" % (1 + i)], ["th%d" % i], "s")
             nx = hs[i + 1] if i < 3 else "hx"
             pick(nx, T[hs[i]][:, 0:C + 2], lambda a, b: T.lhoff[:, i * KW + a:i * KW + b],
                  [hs[i], hs[i] + "s", hs[i] + "e", "lhoff%d" % i], nx, cut)
-        c1, e1 = scan(T.hx[:], C, "hx", "patf")
-        ts(lst("foff"), e1, T.corr[:, 0:1], ADD, [c1, "corr"], ["lfoff"])
-        extra(7)
+        job = (T.hx[:], C, "hx", lst("foff"), "lfoff", "patf")
+        if rd == 0:
+            ring(7, [job])
+            s0, s1 = places(8)
+        else:
+            wraps([job])
         for b in range(8, -1, -1):
             cp(T.fl[:, 32 * b:32 * b + 32], T.fl[:, 32 * b + 32:C + 2].indirect(T.lfoff[:, 2 * b:2 * b + 2]), ["fl", "fle", "lfoff"], ["fl"])
-        extra(8)
-        if rd == 0:
-            ring_end()
+            if rd == 0 and b == 6:
+                last = scan(T.oo[:, s0:s1], s1 - s0, "oo")
+            if rd == 0 and b == 5:
+                ts(T.lordo[:, 0:2], last[1], T.corr[:, 0:1], ADD, [last[0], "corr"], ["lordo"])
+            if rd == 0 and b == 3:
+                cp(T.r1[:, 0:C].indirect(T.lordo[:, 0:KW]), T.iom[:], ["iom", "lordo"], ["r1"])
+            if rd == 0 and b == 2:
+                last = scan(T.r1[:], C, "r1")
+            if rd == 0 and b == 1:
+                ts(lst("poso"), last[1], T.corr[:, 0:1], ADD, [last[0], "corr"], ["lposo"])
         def partner():
             for b in range(4):
                 k = (5, 6, 7, 0)[b]
@@ -454,9 +478,12 @@ def rank_program(g, core, T, topo):
     dma("y", T.oc[:], u8(T.x3q[:]), ["x3"], [])
     for k in range(4):
         dma("s" if k % 2 else "y", T.osc[4 * k:4 * k + 4, :], T.x3sc[32 * k:32 * k + 4, :], ["x3"], [])
-    mm(5, "vq", "vsc", 0, "x3q", "x3sc", ["v", "x3"])
-    cp(T.yf[:], bank(5), ["b5"], ["yf"])
-    dma("s", T.y[:], T.yf[:], ["yf"], [])
+    mm(5, "vq", "vsc", 0, "x3q", "x3sc", ["v", "x3"], 0, HALF)
+    mm(6, "vq", "vsc", 0, "x3q", "x3sc", ["v", "x3"], HALF, C)
+    cp(T.yf[:, 0:HALF], T.ps[:, 2560:2560 + HALF], ["b5"], ["yf"])
+    cp(T.yf[:, HALF:C], T.ps[:, 3072:3072 + HALF], ["b6"], ["yfs"], "s")
+    dma("y", T.y[:, 0:HALF], T.yf[:, 0:HALF], ["yf"], [])
+    dma("s", T.y[:, HALF:C], T.yf[:, HALF:C], ["yfs"], [])
     for s in dsems:
         Q["y"].wait_ge(T.sem[s], 16)
     for q in ("v", "s", "t", "g"):

from concourse.mybir import dt, AluOpType, ActivationFunctionType

C, KW = 288, 18
STEP = (4, 1, 2)
MID = 145
BIG = 512.0
SCAN = "float16"
EARLY = (0, 1)
CUT = 10

SCRATCH = {}
for _n in ("xin", "xt", "zt", "th", "tp", "tu", "gv", "hh"):
    SCRATCH[_n] = ("sbuf", [128, 4 * C], "bfloat16")
for _n in ("ut", "vt"):
    SCRATCH[_n] = ("sbuf", [128, 512], "bfloat16")
SCRATCH["et"] = ("sbuf", [128, 520], "bfloat16")
for _n, _w in (("x0", C), ("x1", C), ("x2", C), ("x3", C), ("p0", C), ("p1", C), ("p2", C), ("z", C),
               ("u", 128), ("ur", 128), ("v", 128), ("e", 512), ("w", 512)):
    SCRATCH[_n + "q"] = ("sbuf", [128, _w], "float8_e4m3fn_x4")
    SCRATCH[_n + "sc"] = ("sbuf", [128, _w], "uint8")
for _n in ("iota", "win", "h1", "h2", "h4", "h8", "fl"):
    SCRATCH[_n] = ("sbuf", [128, 304], "bfloat16")
for _n in ("iom", "pat", "patf", "pp", "r1", "r2", "r3", "hx", "nf", "fo", "sa", "sb", "br", "uda", "udb", "mtr", "mr", "oo"):
    SCRATCH[_n] = ("sbuf", [128, C], "bfloat16")
SCRATCH["hpr"] = ("sbuf", [128, 9 * C], "bfloat16")
for _n in ("c0", "c1", "c2", "c3"):
    SCRATCH[_n] = ("sbuf", [128, C], SCAN)
SCRATCH["pati"] = ("sbuf", [128, C], "int32")
for _n in ("ivl", "mtl", "udl", "hpl"):
    SCRATCH[_n] = ("sbuf", [128, KW], "int32")
SCRATCH["qi"] = ("sbuf", [128, 8], "int32")
for _n in ("corr", "thr", "qz"):
    SCRATCH[_n] = ("sbuf", [128, 8], "float32")
for _n in ("k16", "kb", "jw", "mtw", "dtw", "t1", "t3", "bj", "dj", "tf", "diw", "di2"):
    SCRATCH[_n] = ("sbuf", [128, KW], "float32")
for _n in ("jw2", "im0", "im1", "ta", "tb", "nim", "fm0", "fm1", "fmo"):
    SCRATCH[_n] = ("sbuf", [128, 2 * KW], "float32")
LOCAL = ("iv0", "mi", "mto", "udo", "wino", "off1", "poso", "tauo", "udi")
SCRATCH["lloc"] = ("sbuf", [128, len(LOCAL) * KW], "uint16")
for _n in ("iv1", "iv2", "iv3", "bo0", "bo1", "bo2", "eo0", "eo1", "eo2",
           "ivp0", "ivp1", "ivp2", "bp0", "bp1", "bp2", "ep0", "ep1", "ep2", "hoff", "foff", "ordo"):
    SCRATCH["l" + _n] = ("sbuf", [128, 4 * KW if _n == "hoff" else KW], "uint16")
SCRATCH["lhp"] = ("sbuf", [128, 8 * KW], "uint16")
SCRATCH["luo"] = ("sbuf", [128, 8], "uint16")
SCRATCH["uoi"] = ("sbuf", [128, 8], "int32")
SCRATCH["udf"] = ("sbuf", [128, C], "float32")
SCRATCH["yf"] = ("sbuf", [128, C], "float32")
SCRATCH["ps"] = ("psum", [128, 4096], "float32")

SEMAPHORES = ["cv", "cs", "ct", "cg", "snt"] + ["d%d" % i for i in range(20)]
SEMAPHORES += ["%s%d" % (a, i) for a in ("rx", "ri", "rb", "re") for i in range(3)]

MUL, ADD, SUB, MAX, MIN = AluOpType.mult, AluOpType.add, AluOpType.subtract, AluOpType.max, AluOpType.min
GT, GE, EQ = AluOpType.is_gt, AluOpType.is_ge, AluOpType.is_equal
COPY, IDENT, SIGN = ActivationFunctionType.Copy, ActivationFunctionType.Identity, ActivationFunctionType.Sign


def relays(topo, src, dst):
    if topo.may_write(src, dst):
        return None
    c = [a for a in topo.cores_of(src) if a != src and topo.may_write(a, dst)]
    near = [a for a in c if topo.die(a) == topo.die(src)]
    far = [a for a in c if topo.die(a) != topo.die(src)]
    return (near + far)[:2]


def rank_program(g, core, T, topo):
    rank = T.rank_of(core)
    sent = [0]

    def put(dst, out, in_, sem):
        e = topo.engines(core, dst)[:8]
        rid, pid = topo.addr(dst, core)
        m = 0
        for a in e:
            m |= 1 << a
        g.remote_dma(out, in_, T.sem[sem], T.sem.snt, pid, rid, m)
        sent[0] += len(e)
        return len(e)

    def width(a, b):
        return len(topo.engines(a, b)[:8])

    def u8(ap):
        return ap.bitcast(dt.uint8)

    HALF = C // 2
    if rank is None:
        for rd, step in enumerate(STEP):
            for r, src in enumerate(T.cores):
                dst = T.cores[r ^ step]
                rel = relays(topo, src, dst)
                if not rel or core not in rel:
                    continue
                n = width(src, core)
                if core == rel[0]:
                    g.wait_ge(T.sem["rx%d" % rd], 2 * n)
                    put(dst, u8(T["p%dq" % rd][:, 0:HALF]), u8(T["p%dq" % rd][:, 0:HALF]), "rx%d" % rd)
                    put(dst, T["p%dsc" % rd][:], T["p%dsc" % rd][:], "rx%d" % rd)
                else:
                    g.wait_ge(T.sem["rx%d" % rd], n)
                    put(dst, u8(T["p%dq" % rd][:, HALF:C]), u8(T["p%dq" % rd][:, HALF:C]), "rx%d" % rd)
                    for s, b in (("ri", "livp"), ("rb", "lbp"), ("re", "lep")):
                        g.wait_ge(T.sem["%s%d" % (s, rd)], n)
                        put(dst, T["%s%d" % (b, rd)][:], T["%s%d" % (b, rd)][:], "%s%d" % (s, rd))
        if sent[0]:
            g.wait_ge(T.sem.snt, sent[0])
        return

    Q = {"v": g.vector, "s": g.scalar, "t": g.tensor, "g": g, "y": g.sync}
    SEM = {"v": "cv", "s": "cs", "t": "ct", "g": "cg"}
    cnt = {"v": 0, "s": 0, "t": 0, "g": 0}
    clock = {q: {} for q in Q}
    wr, rdr = {}, {}
    nd = [0]
    dsems = []

    def sync(q, reads, writes):
        need = []
        for k in reads:
            if k in wr:
                need.append(wr[k])
        for k in writes:
            if k in wr:
                need.append(wr[k])
            need += rdr.get(k, [])
        need.sort(key=lambda t: -t[1])
        for sem, val, clk in need:
            if clock[q].get(sem, 0) < val:
                Q[q].wait_ge(T.sem[sem], val)
                for a, b in clk.items():
                    if clock[q].get(a, 0) < b:
                        clock[q][a] = b

    def done(q, sem, val, reads, writes):
        clk = dict(clock[q])
        clk[sem] = val
        tok = (sem, val, clk)
        for k in reads:
            rdr.setdefault(k, []).append(tok)
        for k in writes:
            wr[k] = tok
            rdr[k] = []

    def op(q, call, reads, writes):
        sync(q, reads, writes)
        i = call(Q[q])
        cnt[q] += 1
        i.then_inc(T.sem[SEM[q]], 1)
        done(q, SEM[q], cnt[q], reads, writes)

    def dma(q, out, in_, reads, writes):
        sem = "d%d" % nd[0]
        nd[0] += 1
        sync(q, reads, writes)
        Q[q].dma_start(out, in_).then_inc(T.sem[sem], 16)
        dsems.append(sem)
        done(q, sem, 16, reads, writes)

    def tt(out, a, b, o, reads, writes):
        op("v", lambda e: e.tensor_tensor(out, a, b, o), reads, writes)

    def ts(out, a, s1, o1, reads, writes, s2=None, o2=None):
        if o2 is None:
            op("v", lambda e: e.tensor_scalar(out, a, s1, None, o1), reads, writes)
        else:
            op("v", lambda e: e.tensor_scalar(out, a, s1, s2, o1, o2), reads, writes)

    def cp(out, in_, reads, writes, q="v"):
        if q == "v":
            op("v", lambda e: e.tensor_copy(out, in_), reads, writes)
        else:
            op("s", lambda e: e.activation(out, in_, COPY), reads, writes)

    def pick(out, win, off, reads, key, k=CUT):
        if k < KW:
            op("s", lambda e: e.activation(T[out][:, 16 * k:C], win.indirect(off(k, KW)), COPY), reads, [key + "s"])
        op("v", lambda e: e.tensor_copy(T[out][:, 0:16 * k], win.indirect(off(0, k))), reads, [key])

    rot = [0]

    def scan(row, n, key, pat="pat"):
        b = "c%d" % (rot[0] % 4)
        rot[0] += 1
        op("v", lambda e: e.tensor_tensor_scan(T[b][:, 0:n], row, T[pat][:, 0:n], -2 * BIG, MAX, ADD),
           [key, key + "s", pat], [b])
        return b, T[b][:, 15:n:16]

    def wraps(jobs):
        es = [scan(j[0], j[1], j[2], j[5] if len(j) > 5 else "pat") for j in jobs]
        for (b, e), j in zip(es, jobs):
            ts(j[3], e, T.corr[:, 0:1], ADD, [b, "corr"], [j[4]])

    def wrap(*job):
        wraps([job])

    def lst(name, a=0, b=KW):
        if name in LOCAL:
            o = KW * LOCAL.index(name)
            return T.lloc[:, o + a:o + b]
        return T["l" + name][:, a:b]

    dma("s", T.hpl[:], T.hp[:], [], ["hpl"])
    dma("y", T.ut[:], T.u[:], [], ["ut"])
    dma("s", T.ivl[:], T.iv[:], [], ["ivl"])
    dma("s", T.mtl[:], T.mt[:], [], ["mtl"])
    dma("y", T.xin[:], T.x[:], [], ["xin"])
    dma("s", T.udl[:], T.ud[:], [], ["udl"])
    dma("y", u8(T.wq[:]), T.wc[:], [], ["wq"])
    dma("y", T.wsc[:], T.ws[:], [], ["wsc"])
    dma("y", T.vt[:], T.v[:], [], ["vt"])

    op("v", lambda e: e.memset(T.lordo[:], C - 1), [], ["lordo"])
    op("g", lambda e: e.iota(T.qi[:], [[0, 8]], 0, 1), [], ["qi"])
    op("g", lambda e: e.iota(T.pati[:], [[1, C]], 1024, -1), [], ["pati"])
    op("g", lambda e: e.iota(T.iota[:], [[1, 304]], -MID, 0, allow_small_or_imprecise_dtypes=True), [], ["iota"])
    op("v", lambda e: e.memset(T.et[:], 0.5), [], ["et"])
    op("g", lambda e: e.iota(T.k16[:], [[16, KW]], 0, 0, allow_small_or_imprecise_dtypes=True), [], ["k16"])
    op("g", lambda e: e.iota(T.kb[:], [[-32, KW // 2], [0, 2]], -32, 0, allow_small_or_imprecise_dtypes=True), [], ["kb"])
    op("g", lambda e: e.iota(T.uoi[:], [[16, 8]], 0, 0), [], ["uoi"])
    op("g", lambda e: e.iota(T.iom[:], [[1, C]], -1 - MID, 0, allow_small_or_imprecise_dtypes=True), [], ["iom"])
    op("g", lambda e: e.affine_select(T.et[:], T.et[:], [[1, 520]], EQ, 0.0, -3, -4), ["et"], ["et"])
    ts(T.qi[:], T.qi[:], 15, AluOpType.bitwise_and, ["qi"], ["qi"])
    ts(T.qz[:], T.qi[:], 0.0, EQ, ["qi"], ["qz"])
    ts(T.corr[:], T.qz[:], 2 * BIG, MUL, ["qz"], ["corr"], MID - BIG, ADD)
    ts(T.pati[:], T.pati[:], 15, AluOpType.bitwise_and, ["pati"], ["pati"])
    ts(T.pat[:], T.pati[:], 0.0, EQ, ["pati"], ["pat"], BIG, MUL)
    ts(T.hx[:], T.pati[:], 15.0, EQ, ["pati"], ["hx"], -2 * BIG, MUL)
    cp(T.lhp[:, 0:KW], T.hpl[:], ["hpl"], ["lhp0"])
    cp(T.hpr[:, 0:C], T.iota[:, 0:C].indirect(T.lhp[:, 0:KW]), ["iota", "lhp0"], ["hpr0"], "s")
    tt(T.pat[:], T.pat[:], T.hx[:], ADD, ["pat", "hx"], ["pat"])
    cp(lst("iv0"), T.ivl[:], ["ivl"], ["liv0"])
    cp(lst("mto"), T.mtl[:], ["mtl"], ["lmto"])
    ts(T.thr[:], T.qz[:], -4 * BIG, MUL, ["qz"], ["thr"], 1.5 + 2 * BIG, ADD)
    cp(T.jw[:, 0:1], T.qi[:, 0:1], ["qi"], ["jwq"])
    ts(T.jw2[:, 0:KW], T.k16[:], T.jw[:, 0:1], ADD, ["k16", "jwq"], ["jwa"])
    ts(T.jw2[:, KW:2 * KW], T.k16[:], T.jw[:, 0:1], ADD, ["k16", "jwq"], ["jwb"])
    JW = T.jw2[:, 0:KW]
    JK = ["jwa", "jwb"]

    def square(k):
        if k < 8:
            cp(T.hpr[:, (k + 1) * C:(k + 2) * C], T.hpr[:, k * C:(k + 1) * C].indirect(T.lhp[:, k * KW:(k + 1) * KW]),
               ["hpr%d" % k, "lhp%d" % k], ["hpr%d" % (k + 1)], "s")

    def places(k):
        a, b = (16, 18) if k < 6 or k == 8 else (14, 18) if k == 6 else (10, 18)
        o = 0 if k == 8 else 16 * a - (1 << k)
        if k == 0:
            cp(T.oo[:, 256:C], T.hpr[:, 0:C].indirect(T.lordo[:, a:b]), ["hpr0", "lordo"], ["oo"], "s")
            cp(T.oo[:, 255:C - 1], T.hpr[:, C:2 * C].indirect(T.lordo[:, a:b]), ["hpr1", "lordo", "oo"], ["oo"], "s")
        else:
            cp(T.oo[:, o:o + 16 * (b - a)], T.hpr[:, k * C:(k + 1) * C].indirect(T.lordo[:, a:b]), ["hpr%d" % k, "lordo"], ["oo"], "s")
        return (256, 288) if k < 5 else (o, o + 16 * (b - a))

    def ring(k, jobs=()):
        jobs = list(jobs)
        square(k)
        s0, s1 = places(k)
        if k < 7:
            jobs.append((T.hpr[:, (k + 1) * C:(k + 2) * C], C, "hpr%d" % (k + 1), T.lhp[:, (k + 1) * KW:(k + 2) * KW],
                         "lhp%d" % (k + 1)))
        jobs.append((T.oo[:, s0:s1], s1 - s0, "oo", T.lordo[:, s0 // 16:s1 // 16], "lordo"))
        wraps(jobs)

    op("v", lambda e: e.tensor_copy(T.luo[:], T.uoi[:]), ["uoi"], ["luo"])
    op("v", lambda e: e.memset(T.fm0[:], 0.0), [], ["fm0"])
    op("v", lambda e: e.memset(T.fl[:, C + 1:C + 2], 0.0), [], ["fle"])
    op("v", lambda e: e.memset(T.fl[:, C:C + 1], 1.0), [], ["fl"])
    cp(T.patf[:], T.pat[:], ["pat"], ["patf"])
    tt(T.patf[:, 15:C:16], T.pat[:, 15:C:16], T.kb[:], ADD, ["pat", "kb", "patf"], ["patf"])
    cp(T.im0[:, 0:KW], T.ivl[:], ["ivl"], ["im0"])
    cp(T.mtw[:], T.mtl[:], ["mtl"], ["mtw"])
    ring(0)
    cp(T.mtr[:], T.iota[:, 0:C].indirect(lst("mto")), ["iota", "lmto"], ["mtr"], "s")
    cp(T.mr[:], T.mtr[:].indirect(lst("iv0")), ["mtr", "liv0"], ["mr"], "s")
    tt(T.dtw[:], T.mtw[:], JW, SUB, ["mtw"] + JK, ["dtw"])
    cp(lst("udi"), T.udl[:], ["udl"], ["ludi"])

    def prepare(rd):
        im = "im%d" % (rd % 2)
        b, e = scan(T.mr[:], C, "mr")
        ts(T[im][:, KW:2 * KW], e, T.corr[:, 0:1], ADD, [b, "corr"], [im + "m"])
        cp(lst("mi"), T[im][:, KW:2 * KW], [im + "m"], ["lmi"])
        tt(T.ta[:], T[im][:], T.jw2[:], GT, [im, im + "m"] + JK, ["ta"])
        ts(T.tb[:], T[im][:], float(C + 1), SUB, [im, im + "m"], ["tb"])
        tt(T.diw[:], T[im][:, KW:2 * KW], T[im][:, 0:KW], SUB, [im, im + "m"], ["diw"])
        tt(T.nim[:], T.ta[:], T.tb[:], MUL, ["ta", "tb"], ["nim"])
        tt(T.fm0[:, 1:2 * KW:2], T.nim[:, KW:2 * KW], T.nim[:, 0:KW], SUB, ["nim"], ["fm0"])
        ts(T.fm1[:, 1:2 * KW:2], T.nim[:, 0:KW], float(C + 1), ADD, ["nim"], ["fm1"])

    for b in ("win", "h1", "h2", "h4", "h8"):
        cp(T[b][:, C:C + 2], T.iota[:, C:C + 2], ["iota"], [b + "e"])
    op("v", lambda e: e.memset(T.iom[:, 0:1], float(C - 1 - MID)), ["iom"], ["iom"])
    op("v", lambda e: e.quantize_mx(T.uq[:], T.usc[:], T.ut[:]), ["ut"], ["u"])
    op("v", lambda e: e.tensor_copy(T.urq[:, 0:128].bitcast(dt.uint32), T.uq[:, 0:128].bitcast(dt.uint32).indirect(T.luo[:, 0:8])),
       ["u", "luo"], ["urq"])
    op("s", lambda e: e.activation(T.ursc[:, 0:128], T.usc[:, 0:128].indirect(T.luo[:, 0:8]), COPY), ["u", "luo"], ["ursc"])
    prepare(0)
    op("v", lambda e: e.quantize_mx(T.x0q[:], T.x0sc[:], T.xin[:]), ["xin"], ["x0"])
    ring(1)

    def mm(bank, l, ls, a, r, rs, reads, c=0, d=C):
        op("t", lambda e: e.matmul_mx(T.ps[:, 512 * bank:512 * bank + d - c], T[l][:, a:a + 128], T[ls][:, a:a + 128], T[r][:, c:d],
                                      T[rs][:, c:d], True, True), reads, ["b%d" % bank])

    def bank(k):
        return T.ps[:, 512 * k:512 * k + C]

    def pl(name, b):
        return T[name][:, b * C:(b + 1) * C]

    def constants(b):
        op("v", lambda e: e.quantize_mx(T.eq[:, 128 * b:128 * b + 128], T.esc[:, 128 * b:128 * b + 128], T.et[:, 3 - b:515 - b]),
           ["et"], ["e%d" % b])

    ud = ["uda", "udb"]
    for rd, step in enumerate(STEP):
        xq, xs = "x%dq" % rd, "x%dsc" % rd
        dst = T.cores[rank ^ step]
        rel = relays(topo, core, dst)
        backrel = relays(topo, dst, core)
        RX, RI, RB, RE = ["%s%d" % (a, rd) for a in ("rx", "ri", "rb", "re")]
        pq, pks = "p%dq" % rd, "p%dsc" % rd

        def extra(k):
            if rd == 0:
                ring(k)

        sync("g", ["x%d" % rd], [])
        if rel:
            put(rel[0], u8(T[pq][:, 0:HALF]), u8(T[xq][:, 0:HALF]), RX)
            put(rel[1], u8(T[pq][:, HALF:C]), u8(T[xq][:, HALF:C]), RX)
            put(rel[0], T[pks][:], T[xs][:], RX)
        else:
            put(dst, u8(T[pq][:]), u8(T[xq][:]), RX)
            put(dst, T[pks][:], T[xs][:], RX)
        listto = rel[1] if rel else dst
        if backrel:
            wr["p%d" % rd] = (RX, 2 * width(backrel[0], core) + width(backrel[1], core), {})
            nl = width(backrel[1], core)
        else:
            wr["p%d" % rd] = (RX, 2 * width(dst, core), {})
            nl = width(dst, core)
        wr["livp%d" % rd] = (RI, nl, {RI: nl})
        wr["lbp%d" % rd] = (RB, nl, {RB: nl})
        wr["lep%d" % rd] = (RE, nl, {RE: nl})
        wr["p%d" % rd][2][RX] = wr["p%d" % rd][1]

        mm(0, "urq", "ursc", 0, xq, xs, ["urq", "ursc", "x%d" % rd], 0, HALF)
        mm(5, "urq", "ursc", 0, xq, xs, ["urq", "ursc", "x%d" % rd], HALF, C)
        ts(T.pp[:, 0:HALF], T.ps[:, 0:HALF], 0.0, GT, ["b0"], ["pp"])
        if rd == 0:
            constants(0)
            constants(1)
        op("s", lambda e: e.activation(T.pp[:, HALF:C], T.ps[:, 2560:2560 + HALF], SIGN), ["b5"], ["pps"])
        cp(T.r1[:], T.pp[:].indirect(lst("iv%d" % rd)), ["pp", "pps", "liv%d" % rd], ["r1"], "s")
        cp(T.r3[:], T.pp[:].indirect(lst("mto")), ["pp", "pps", "lmto"], ["r3"], "s")
        cp(T.r2[:], T.pp[:].indirect(lst("mi")), ["pp", "pps", "lmi"], ["r2"])
        c2, e2 = scan(T.r2[:], C, "r2")
        c1, e1 = scan(T.r1[:], C, "r1")
        tt(T.t1[:], e1, e2, ADD, [c1, c2], ["t1"])
        ts(T.fm1[:, 0:2 * KW:2], T.t1[:], T.thr[:, 0:1], GE, ["t1", "thr"], ["bo"])
        op("v", lambda e: e.tensor_tensor_scan(T.fmo[:], T.fm0[:], T.fm1[:], 0.0, MUL, ADD), ["bo", "fm0", "fm1"], ["fmo"])
        tw = T.fmo[:, 1:2 * KW:2]
        cp(lst("wino"), tw, ["fmo"], ["lwino"])
        op("s", lambda e: e.activation(T.win[:, 96:C], T.iota[:, 0:C + 2].indirect(lst("wino", 6, KW)), COPY), ["iota", "lwino"], ["wins"])
        ts(lst("off1"), tw, float(C), MIN, ["fmo"], ["loff1"])
        cp(T.win[:, 0:96], T.iota[:, 0:C + 2].indirect(lst("wino", 0, 6)), ["iota", "lwino"], ["win"])
        imo, imn = "im%d" % (rd % 2), "im%d" % ((rd + 1) % 2)
        tt(T.di2[:], T.fm1[:, 0:2 * KW:2], T.diw[:], MUL, ["bo", "diw"], ["di2"])
        tt(T[imn][:, 0:KW], T.di2[:], T[imo][:, 0:KW], ADD, ["di2", imo], [imn])
        cp(lst("iv%d" % (rd + 1)), T[imn][:, 0:KW], [imn], ["liv%d" % (rd + 1)])
        sync("g", ["liv%d" % (rd + 1)], [])
        put(listto, T["livp%d" % rd][:], T["liv%d" % (rd + 1)][:], RI)
        if rd == 0:
            constants(2)
            constants(3)
        for b in range(4):
            mm(1 + b, "eq", "esc", 128 * b, xq, xs, ["e%d" % b, "x%d" % rd])
        cut = CUT if rd else KW
        extra(2)
        if rd == 0:
            cp(T.uda[:], T.iota[:, 0:C].indirect(lst("udi")), ["iota", "ludi"], ["uda"], "s")
        pick("h1", T.win[:, 0:C + 2], lambda a, b: lst("off1", a, b), ["win", "wins", "wine", "loff1"], "h1", cut)
        hs = ["h1", "h2", "h4", "h8"]
        for i in range(4):
            of = T.lhoff[:, i * KW:(i + 1) * KW]
            job = (T[hs[i]][:, 0:C], C, hs[i], of, "lhoff%d" % i)
            if rd == 0:
                ring(3 + i, [job])
            else:
                wraps([job])
            cp(pl("th", i), bank(1 + i), ["b%d" % (1 + i)], ["th%d" % i], "s")
            nx = hs[i + 1] if i < 3 else "hx"
            pick(nx, T[hs[i]][:, 0:C + 2], lambda a, b: T.lhoff[:, i * KW + a:i * KW + b],
                 [hs[i], hs[i] + "s", hs[i] + "e", "lhoff%d" % i], nx, cut)
        job = (T.hx[:], C, "hx", lst("foff"), "lfoff", "patf")
        if rd == 0:
            ring(7, [job])
            s0, s1 = places(8)
        else:
            wraps([job])
        for b in range(8, -1, -1):
            cp(T.fl[:, 32 * b:32 * b + 32], T.fl[:, 32 * b + 32:C + 2].indirect(T.lfoff[:, 2 * b:2 * b + 2]), ["fl", "fle", "lfoff"], ["fl"])
            if rd == 0 and b == 6:
                last = scan(T.oo[:, s0:s1], s1 - s0, "oo")
            if rd == 0 and b == 5:
                ts(T.lordo[:, 0:2], last[1], T.corr[:, 0:1], ADD, [last[0], "corr"], ["lordo"])
            if rd == 0 and b == 3:
                cp(T.r1[:, 0:C].indirect(T.lordo[:, 0:KW]), T.iom[:], ["iom", "lordo"], ["r1"])
            if rd == 0 and b == 2:
                last = scan(T.r1[:], C, "r1")
            if rd == 0 and b == 1:
                ts(lst("poso"), last[1], T.corr[:, 0:1], ADD, [last[0], "corr"], ["lposo"])
        def partner():
            for b in range(4):
                k = (5, 6, 7, 0)[b]
                mm(k, "eq", "esc", 128 * b, pq, pks, ["e%d" % b, "p%d" % rd])
                cp(pl("tp", b), bank(k), ["b%d" % k], ["tp%d" % b], "s")

        if rd in EARLY:
            partner()
        op("s", lambda e: e.activation(T.nf[:], T.fl[:, 0:C].indirect(lst("ordo")), IDENT, bias=1.0, scale=-1.0), ["fl", "lordo"], ["nf"])
        tt(T.fo[:], T.fl[:, 0:C].indirect(lst("ordo")), T.oo[:], MUL, ["fl", "lordo", "oo"], ["fo"])
        op("v", lambda e: e.tensor_tensor_scan(T.sb[:], T.nf[:], T.fo[:], 0.0, MUL, ADD), ["nf", "fo"], ["sb"])
        pick("br", T.sb[:], lambda a, b: lst("poso", a, b), ["sb", "lposo"], "br")
        wrap(T.br[:], C, "br", lst("bo%d" % rd), "lbo%d" % rd)
        sync("g", ["lbo%d" % rd], [])
        put(listto, T["lbp%d" % rd][:], T["lbo%d" % rd][:], RB)
        if rd not in EARLY:
            partner()
        def past(b):
            cp(pl("gv", b), pl("tp", b).indirect(lst("ivp%d" % rd)), ["tp%d" % b, "livp%d" % rd], ["gv%d" % b], "s")

        past(0)
        past(1)
        c1, e1 = scan(T.pp[:], C, "pp")
        c2, e2 = scan(T.r3[:], C, "r3")
        tt(T.t3[:], e1, e2, ADD, [c1, c2], ["t3"])
        ts(T.bj[:], T.t3[:], T.thr[:, 0:1], GE, ["t3", "thr"], ["bj"])
        tt(T.dj[:], T.bj[:], T.dtw[:], MUL, ["bj", "dtw"], ["dj"])
        tt(T.tf[:], T.dj[:], JW, ADD, ["dj"] + JK, ["tf"])
        cp(lst("tauo"), T.tf[:], ["tf"], ["ltauo"])
        uo, un = ud[rd % 2], ud[(rd + 1) % 2]
        cp(T[un][:], T[uo][:].indirect(lst("tauo")), [uo, "ltauo"], [un], "s")
        past(2)
        past(3)
        cp(T.r2[:], T.br[:].indirect(lst("ivp%d" % rd)), ["br", "brs", "livp%d" % rd], ["r2"])
        wrap(T.r2[:], C, "r2", lst("eo%d" % rd), "leo%d" % rd)
        sync("g", ["leo%d" % rd], [])
        put(listto, T["lep%d" % rd][:], T["leo%d" % rd][:], RE)
        wrap(T[un][:], C, un, lst("udo"), "ludo")
        for b in range(4):
            cp(pl("tu", b), pl("th", b).indirect(lst("udo")), ["th%d" % b, "ludo"], ["tu%d" % b], "s")
        if rd < 2:
            cp(T.mr[:], T.mtr[:].indirect(lst("iv%d" % (rd + 1))), ["mtr", "liv%d" % (rd + 1)], ["mr"], "s")
        for b in range(4):
            tt(T.zt[:, b:4 * C:4], pl("tp", b).indirect(lst("bp%d" % rd)), pl("gv", b), ADD,
               ["tp%d" % b, "gv%d" % b, "lbp%d" % rd], ["zt%d" % b])
        op("v", lambda e: e.quantize_mx(T.zq[:], T.zsc[:], T.zt[:]), ["zt%d" % b for b in range(4)], ["z"])
        for b in range(4):
            mm(1 + b, "wq", "wsc", 128 * b, "zq", "zsc", ["wq", "wsc", "z"])
        for b in range(4):
            op("s", lambda e: e.activation(pl("hh", b), bank(1 + b), COPY, scale=0.015625), ["b%d" % (1 + b)], ["hh%d" % b])
        if rd < 2:
            prepare(rd + 1)
        else:
            op("s", lambda e: e.activation(T.udf[:], T[un][:], COPY, bias=float(MID)), [un], ["udf"])
            dma("y", T.uo[:], T.udf[0:128:16, :], ["udf"], [])
            op("v", lambda e: e.quantize_mx(T.vq[:], T.vsc[:], T.vt[:]), ["vt"], ["v"])
        for b in range(4):
            tt(T.xt[:, b:4 * C:4], pl("hh", b).indirect(lst("ep%d" % rd)), pl("tu", b), ADD,
               ["hh%d" % b, "tu%d" % b, "lep%d" % rd], ["xt%d" % b])
        nq = rd + 1
        op("v", lambda e: e.quantize_mx(T["x%dq" % nq][:], T["x%dsc" % nq][:], T.xt[:]), ["xt%d" % b for b in range(4)], ["x%d" % nq])

    dma("y", T.oc[:], u8(T.x3q[:]), ["x3"], [])
    for k in range(4):
        dma("s" if k % 2 else "y", T.osc[4 * k:4 * k + 4, :], T.x3sc[32 * k:32 * k + 4, :], ["x3"], [])
    mm(5, "vq", "vsc", 0, "x3q", "x3sc", ["v", "x3"], 0, HALF)
    mm(6, "vq", "vsc", 0, "x3q", "x3sc", ["v", "x3"], HALF, C)
    cp(T.yf[:, 0:HALF], T.ps[:, 2560:2560 + HALF], ["b5"], ["yf"])
    cp(T.yf[:, HALF:C], T.ps[:, 3072:3072 + HALF], ["b6"], ["yfs"], "s")
    dma("y", T.y[:, 0:HALF], T.yf[:, 0:HALF], ["yf"], [])
    dma("s", T.y[:, HALF:C], T.yf[:, HALF:C], ["yfs"], [])
    for s in dsems:
        Q["y"].wait_ge(T.sem[s], 16)
    for q in ("v", "s", "t", "g"):
        g.wait_ge(T.sem[SEM[q]], cnt[q])
    g.wait_ge(T.sem.snt, sent[0])
